import numpy as np
import ml_dtypes


def mxq(x, axis, fmt="e4m3"):
    dtype, down = {"e4m3": (ml_dtypes.float8_e4m3fn, 7), "e5m2": (ml_dtypes.float8_e5m2, 14)}[fmt]
    v = np.moveaxis(np.asarray(x, np.float32).astype(ml_dtypes.bfloat16).astype(np.float64), axis, -1)
    blocks = v.reshape(v.shape[:-1] + (-1, 32))
    amax = np.abs(blocks).max(-1, keepdims=True)
    byte = np.maximum(np.where(amax > 0, np.frexp(amax)[1] - 1 + 127, 0) - down, 1)
    scale = np.exp2(byte - 127.0)
    codes = (blocks / scale).astype(np.float32).astype(dtype).astype(np.float64)
    return np.moveaxis((codes * scale).reshape(v.shape), -1, axis)


WIDE = False


def mx_kscale(k):
    if not WIDE:
        return np.ones(k)
    levels = np.array([10, -10, 5, -5, 0])
    if k % 512:
        return np.exp2(np.random.permutation(np.resize(levels, k // 32))).repeat(32)
    a = np.empty((k // 512, 16))
    for p in range(k // 512):
        a[p, :8] = np.random.permutation(np.resize(levels, 8))
        for g in range(8):
            far = levels[np.abs(levels - a[p, g]) >= 10]
            a[p, g + 8] = far[np.random.randint(len(far))]
    return np.exp2(a.ravel()).repeat(32)


def f64(x):
    return np.asarray(x).astype(np.float64)


def striped(idx):
    return np.tile(idx.reshape(-1, 16).T, (8, 1)).astype(np.uint16)


def unstriped(offs):
    return offs[:16].T.reshape(-1).astype(np.int64)


E2M1 = np.array([0.0, 0.5, 1.0, 1.5, 2.0, 3.0, 4.0, 6.0, -0.0, -0.5, -1.0, -1.5, -2.0, -3.0, -4.0, -6.0])


def pack_weight(w, fmt):
    k, n = w.shape
    w = f64(np.asarray(w, np.float32).astype(ml_dtypes.bfloat16)).reshape(k // 32, 32, n)
    amax = np.abs(w).max(1)
    if fmt == "e4m3":
        byte = np.frexp(amax)[1] - 1 + 127 - 7
    else:
        mant, ex = np.frexp(amax / 6.0)
        byte = np.where(mant > 0.5, ex, ex - 1) + 127
    byte = np.clip(np.where(amax > 0, byte, 1), 1, 254)
    scaled = (w * np.exp2(127.0 - byte)[:, None, :]).reshape(k, n).astype(np.float32)
    by_word = np.ascontiguousarray(scaled.reshape(k // 512, 128, 4, n).transpose(0, 1, 3, 2))
    if fmt == "e4m3":
        words = by_word.astype(ml_dtypes.float8_e4m3fn).view(np.uint8)
    else:
        c = by_word.astype(ml_dtypes.float4_e2m1fn).view(np.uint8) & 0xF
        words = (c[..., 0::2] | (c[..., 1::2] << 4)).reshape(k // 512, 128, 2 * n)
    return np.ascontiguousarray(words), np.ascontiguousarray(byte.astype(np.uint8).reshape(k // 512, 16, n))


def unpack_weight(words, scales, fmt):
    g, _, n = scales.shape
    words = np.ascontiguousarray(words).reshape(g, 128, n, -1)
    if fmt == "e4m3":
        vals = words.view(ml_dtypes.float8_e4m3fn).astype(np.float64)
    else:
        nib = np.empty((g, 128, n, 4), np.uint8)
        nib[..., 0::2] = words & 0xF
        nib[..., 1::2] = words >> 4
        vals = E2M1[nib]
    vals = vals * np.repeat(np.exp2(scales.astype(np.float64) - 127.0), 8, axis=1)[..., None]
    return vals.transpose(0, 1, 3, 2).reshape(g * 512, n)


def gelu(v):
    return 0.5 * v * (1.0 + np.tanh(np.sqrt(2.0 / np.pi) * (v + 0.044715 * v**3)))


def striped8(idx):
    return np.concatenate([v.reshape(-1, 16).T for v in idx]).astype(np.uint16)


def unstriped8(offs):
    return np.stack([offs[16 * g:16 * g + 16].T.reshape(-1) for g in range(8)]).astype(np.int64)


def heads(xT, wgt, idx8):
    k = np.arange(xT.shape[0])
    return wgt[k // 4 % 128] * xT[k[:, None], idx8[k % 512 // 64]]


K, M, H, N, T, TX, S = 1024, 1024, 1024, 512, 2048, 1024, 512

def setup_inputs():
    n = np.random.standard_normal
    s = mx_kscale(K)[:, None]
    sm = mx_kscale(M)[:, None]
    u = mx_kscale(H)[:, None]
    wgt = np.repeat(np.random.uniform(0.5, 2.0, (8, S)), 16, axis=0)
    picks = np.stack([np.random.permutation(TX)[:S] for _ in range(8)])
    tab_words, tab_scales = pack_weight(n((M, T)) * sm, "e4m3")
    wm_words, wm_scales = pack_weight(0.6 * n((M, H)) / np.sqrt(M) / sm, "e2m1")
    return {
        "xT": (n((K, TX)) * s).astype(np.float32),
        "wgt": wgt.astype(np.float32),
        "offs2": striped8(picks),
        "tab_words": tab_words, "tab_scales": tab_scales,
        "offs": striped(np.random.permutation(T)[:S]),
        "wx": (0.6 * n((K, H)) / np.sqrt(K) / s).astype(np.float32),
        "wm_words": wm_words, "wm_scales": wm_scales,
        "b": (0.3 * n(H)).astype(np.float32),
        "g": (np.exp(0.3 * n(H)) * u[:, 0]).astype(np.float32),
        "wo": (n((H, N)) / np.sqrt(H) / u).astype(np.float32),
        "bo": (0.3 * n(N)).astype(np.float32),
    }

def reference(xT, wgt, offs2, tab_words, tab_scales, offs, wx, wm_words, wm_scales, b, g, wo, bo):
    xg = heads(f64(xT), f64(wgt), unstriped8(offs2))
    v = unpack_weight(tab_words, tab_scales, "e4m3")[:, unstriped(offs)]
    wm = unpack_weight(wm_words, wm_scales, "e2m1")
    z = mxq(f64(wx), 0, "e4m3").T @ mxq(xg, 0, "e4m3") + wm.T @ v
    h = f64(g)[:, None] * np.tanh(z + f64(b)[:, None])
    y = mxq(f64(wo), 0, "e4m3").T @ mxq(h, 0, "e4m3")
    return y + f64(bo)[:, None]

@@ -1,0 +1,307 @@
+from contextlib import ExitStack
+
+import concourse.mybir as mybir
+from concourse.masks import make_identity
+
+K, M, H, N, T, TX, S = 1024, 1024, 1024, 512, 2048, 1024, 512
+FLOPS = 2 * S * (K * H + M * H + H * N)
+
+F32 = mybir.dt.float32
+BF16 = mybir.dt.bfloat16
+I32 = mybir.dt.int32
+U32 = mybir.dt.uint32
+U16 = mybir.dt.uint16
+U8 = mybir.dt.uint8
+FP8X4 = mybir.dt.float8_e4m3fn_x4
+FP4X4 = mybir.dt.float4_e2m1fn_x4
+ALU = mybir.AluOpType
+ACT = mybir.ActivationFunctionType
+
+P = 128
+PACK = 4
+PASS = P * PACK
+PASSES = 2
+HALF = S // 2
+
+
+def tile_list_head_picks_prefix_memory_kernel(
+    tc, xT, wgt, offs2, tab_words, tab_scales, offs, wx, wm_words, wm_scales, b, g, wo, bo, out
+):
+    nc = tc.nc
+    with ExitStack() as ctx:
+        sb = ctx.enter_context(tc.tile_pool(name="sb", bufs=1))
+        psum = ctx.enter_context(tc.psum_pool(name="psum", bufs=1))
+
+        def tile(name, shape, dtype):
+            return sb.tile(shape, dtype, name=name, align_bytes=64)
+
+        def bank(name, index):
+            return psum.tile([P, S], F32, name=name, tag="bank%d" % index)
+
+        def quantize(name, source, columns):
+            codes = tile(name + "_codes", [P, columns], U32)
+            scales = tile(name + "_scales", [P, columns], U8)
+            nc.vector.quantize_mx(out=codes[:].bitcast(FP8X4), scales=scales[:], in_=source[:])
+            return codes, scales
+
+        def interleave(copy, name, planes, columns):
+            woven = tile(name, [P, PACK * columns], BF16)
+            copy(
+                out=woven[:].rearrange("p (c j i) -> p c i j", j=4, i=PACK),
+                in_=planes.rearrange("p i (c j) -> p c i j", j=4),
+            )
+            return woven
+
+        tab_plane = tile("tab_plane", [P, PASSES * T], U8)
+        wm_plane_raw = tile("wm_plane_raw", [P, PASSES * H], U8)
+        rows = tile("rows", [P, PASS], F32)
+        identity = tile("identity", [P, P], F32)
+        make_identity(nc, identity[:])
+        nc.vector.memset(rows[:], 0.0)
+        nc.vector.memset(tab_plane[:].bitcast(I32), 0)
+        nc.vector.memset(wm_plane_raw[:].bitcast(I32), 0)
+        warm = tile("warm", [P, 1], F32)
+        nc.scalar.activation(warm[:], identity[:, 0:1], ACT.Tanh)
+        for q in range(4):
+            nc.gpsimd.dma_start(
+                out=tab_plane[32 * q : 32 * q + 4, :].bitcast(I32).rearrange("r (a c) -> r a c", a=PASSES),
+                in_=tab_scales[:, 4 * q : 4 * q + 4, :].bitcast(I32).rearrange("a r c -> r a c"),
+            )
+
+        head_lists = sb.tile([P, S // 16], U16, name="head_lists")
+        table_list = sb.tile([P, S // 16], U16, name="table_list")
+        weights = tile("weights", [P, S], F32)
+        x_rows = xT.rearrange("(a p i) t -> a i p t", a=PASSES, i=PACK)
+        x_planes = {}
+
+        def load_x(a, i):
+            x_planes[a, i] = tile("x_%d_%d" % (a, i), [P, TX], F32)
+            nc.sync.dma_start(out=x_planes[a, i][:], in_=x_rows[a, i])
+
+        nc.sync.dma_start(head_lists[:], offs2)
+        load_x(0, 0)
+        nc.sync.dma_start(out=weights[:], in_=wgt)
+        load_x(0, 1)
+        nc.sync.dma_start(out=rows[0:2, :], in_=b.rearrange("(h c) -> h c", h=2))
+        nc.sync.dma_start(out=rows[2:4, :], in_=g.rearrange("(h c) -> h c", h=2))
+        nc.sync.dma_start(out=rows[4:5, :], in_=bo.rearrange("(h c) -> h c", h=1))
+        load_x(0, 2)
+        load_x(0, 3)
+        nc.sync.dma_start(table_list[:], offs)
+        for q in range(4):
+            nc.sync.dma_start(
+                out=wm_plane_raw[32 * q : 32 * q + 4, :].bitcast(I32).rearrange("r (a c) -> r a c", a=PASSES),
+                in_=wm_scales[:, 4 * q : 4 * q + 4, :].bitcast(I32).rearrange("a r c -> r a c"),
+            )
+        wm_raw = tile("wm_raw", [P, PASSES * 2 * H], U8)
+        nc.sync.dma_start(
+            out=wm_raw[:].bitcast(I32).rearrange("p (a c) -> p a c", a=PASSES),
+            in_=wm_words.bitcast(I32).rearrange("a p c -> p a c"),
+        )
+        tab = [tile("tab_%d" % a, [P, T], U32) for a in range(PASSES)]
+
+        def load_table(a):
+            nc.sync.dma_start(
+                out=tab[a][:].bitcast(I32), in_=tab_words[a].rearrange("p t i -> p (t i)").bitcast(I32)
+            )
+
+        load_table(0)
+        for i in range(PACK):
+            load_x(1, i)
+        load_table(1)
+        wx_rows = wx.rearrange("(a p i) r -> a p i r", a=PASSES, i=PACK)
+        wx_raw = {}
+        for hb in range(PASSES):
+            for a in range(PASSES):
+                wx_raw[hb, a] = tile("wx_%d_%d" % (hb, a), [P, PACK, PASS], F32)
+                nc.sync.dma_start(out=wx_raw[hb, a][:], in_=wx_rows[a][:, :, hb * PASS : (hb + 1) * PASS])
+        wo_rows = wo.rearrange("(b u t s) n -> b t u s n", b=PASSES, t=PACK, s=4)
+        wo_raw = []
+        for hb in range(PASSES):
+            wo_raw.append(tile("wo_%d" % hb, [P, PACK, N], F32))
+            for t in range(PACK):
+                nc.sync.dma_start(out=wo_raw[hb][:, t, :], in_=wo_rows[hb, t])
+
+        rows_ordered = tile("rows_ordered", [P, PASS], F32)
+        nc.scalar.copy(
+            out=rows_ordered[:].rearrange("p (t u s) -> p u t s", t=PACK, s=4),
+            in_=rows[:].rearrange("p (u t s) -> p u t s", t=PACK, s=4),
+        )
+        turned = bank("turned", 6)
+        turned_bo = bank("turned_bo", 7)
+        for t in range(PACK):
+            nc.tensor.transpose(turned[:, t * P : (t + 1) * P], rows_ordered[:, t * P : (t + 1) * P], identity[:])
+        for c in range(N // P):
+            nc.tensor.transpose(turned_bo[:, c * P : (c + 1) * P], rows[:, c * P : (c + 1) * P], identity[:])
+        per_channel = tile("per_channel", [P, 4 * PACK], F32)
+        nc.scalar.copy(
+            out=per_channel[:].rearrange("p (r t) -> p r t", t=PACK),
+            in_=turned[:].rearrange("p (t r) -> p r t", t=PACK)[:, 0:4, :],
+        )
+        out_bias = tile("out_bias", [P, N // P], F32)
+        nc.scalar.copy(out=out_bias[:], in_=turned_bo[:, 4 : S : P])
+
+        def gather_x(a):
+            picked = tile("picked_%d" % a, [P, PACK, S], F32)
+            for i in range(PACK):
+                nc.vector.tensor_tensor(
+                    picked[:, i, :], x_planes[a, i][:].indirect(head_lists[:]), weights[:], ALU.mult
+                )
+            return interleave(nc.scalar.copy, "xg_bf16_%d" % a, picked[:], S)
+
+        xg_bf16 = [gather_x(0)]
+
+        v_scales = []
+        for a in range(PASSES):
+            v_scales.append(tile("v_scales_%d" % a, [P, S], U8))
+            nc.vector.tensor_copy(v_scales[a][:], tab_plane[:, a * T : (a + 1) * T].indirect(table_list[:]))
+        wm_plane = tile("wm_plane", [P, PASSES * H], U8)
+        nc.vector.tensor_copy(
+            out=wm_plane[:].bitcast(I32).rearrange("p (e t u) -> p e u t", t=PACK, u=32),
+            in_=wm_plane_raw[:].bitcast(I32).rearrange("p (e u t) -> p e u t", t=PACK, u=32),
+        )
+        wm_codes = tile("wm_codes", [P, PASSES * 2 * H], U8)
+        nc.vector.tensor_copy(
+            out=wm_codes[:].bitcast(I32).rearrange("p (e t u w) -> p e u t w", t=PACK, u=32, w=2),
+            in_=wm_raw[:].bitcast(I32).rearrange("p (e u t w) -> p e u t w", t=PACK, u=32, w=2),
+        )
+
+        z = {}
+        for hb in range(PASSES):
+            for t in range(PACK):
+                z[hb, t] = bank("z_%d_%d" % (hb, t), PACK * hb + t)
+
+        def table_passes(a):
+            v_codes = tile("v_codes_%d" % a, [P, S], U32)
+            nc.vector.tensor_copy(v_codes[:], tab[a][:].indirect(table_list[:]))
+            for hb in range(PASSES):
+                for t in range(PACK):
+                    c0 = a * H + hb * PASS + t * P
+                    nc.tensor.matmul_mx(
+                        out=z[hb, t][:],
+                        lhsT=wm_codes[:, 2 * c0 : 2 * (c0 + P)].bitcast(FP4X4),
+                        lhsT_scale=wm_plane[:, c0 : c0 + P],
+                        rhs=v_codes[:].bitcast(FP8X4),
+                        rhs_scale=v_scales[a][:],
+                        start=(a == 0),
+                        stop=False,
+                    )
+
+        table_passes(0)
+        xg = [quantize("xg_0", xg_bf16[0], S)]
+        xg_bf16.append(gather_x(1))
+        table_passes(1)
+        xg.append(quantize("xg_1", xg_bf16[1], S))
+
+        def wx_passes(hb, a, copies):
+            woven = []
+            for pair, copy in enumerate(copies):
+                woven.append(tile("wx_bf16_%d_%d_%d" % (hb, a, pair), [P, 2 * PACK * P], BF16))
+                copy(
+                    out=woven[pair][:].rearrange("p (t u s i) -> p u t i s", t=2, s=4, i=PACK),
+                    in_=wx_raw[hb, a][:].rearrange("p i (u t s) -> p u t i s", t=PACK, s=4)[
+                        :, :, 2 * pair : 2 * pair + 2
+                    ],
+                )
+            for pair in range(2):
+                codes, scales = quantize("wx_%d_%d_%d" % (hb, a, pair), woven[pair], 2 * P)
+                for c in range(2):
+                    nc.tensor.matmul_mx(
+                        out=z[hb, 2 * pair + c][:],
+                        lhsT=codes[:, c * P : (c + 1) * P].bitcast(FP8X4),
+                        lhsT_scale=scales[:, c * P : (c + 1) * P],
+                        rhs=xg[a][0][:].bitcast(FP8X4),
+                        rhs_scale=xg[a][1][:],
+                        start=False,
+                        stop=(a == PASSES - 1),
+                    )
+
+        h = {}
+
+        tanh = {}
+
+        def activate(hb, half):
+            cols = slice(half * HALF, (half + 1) * HALF)
+            th = tile("tanh_%d_%d" % (hb, half), [P, PACK, HALF], F32)
+            for t in range(PACK):
+                nc.scalar.activation(
+                    th[:, t, :], z[hb, t][:, cols], ACT.Tanh, bias=per_channel[:, PACK * hb + t : PACK * hb + t + 1]
+                )
+            tanh[hb, half] = th
+
+        def hidden(hb, half):
+            th = tanh[hb, half]
+            gain = per_channel[:, PACK * (2 + hb) : PACK * (3 + hb)]
+            woven = tile("h_bf16_%d_%d" % (hb, half), [P, PACK * HALF], BF16)
+            nc.vector.tensor_tensor(
+                woven[:].rearrange("p (c j t) -> p c t j", j=4, t=PACK),
+                th[:].rearrange("p t (c j) -> p c t j", j=4),
+                gain.rearrange("p (c t j) -> p c t j", c=1, j=1).to_broadcast([P, HALF // 4, PACK, 4]),
+                ALU.mult,
+            )
+            h[hb, half] = quantize("h_%d_%d" % (hb, half), woven, HALF)
+
+        shared = (nc.vector.tensor_copy, nc.scalar.copy)
+        wx_passes(0, 0, shared)
+        wx_passes(0, 1, shared)
+        wx_passes(1, 0, (nc.vector.tensor_copy, nc.vector.tensor_copy))
+        activate(0, 0)
+        activate(0, 1)
+        wx_passes(1, 1, shared)
+        hidden(0, 0)
+        activate(1, 0)
+        activate(1, 1)
+        hidden(0, 1)
+
+        wo_q = {}
+        y = {}
+        for half in range(2):
+            for pair in range(2):
+                y[half, pair] = bank("y_%d_%d" % (half, pair), 2 * half + pair)
+
+        def wo_quantize(hb, pair, copy):
+            planes = wo_raw[hb][:, :, 2 * P * pair : 2 * P * (pair + 1)]
+            name = "wo_%d_%d" % (hb, pair)
+            wo_q[hb, pair] = quantize(name, interleave(copy, name + "_bf16", planes, 2 * P), 2 * P)
+
+        def y_passes(hb, half, pair):
+            for c in range(2):
+                nc.tensor.matmul_mx(
+                    out=y[half, pair][:, c * HALF : (c + 1) * HALF],
+                    lhsT=wo_q[hb, pair][0][:, c * P : (c + 1) * P].bitcast(FP8X4),
+                    lhsT_scale=wo_q[hb, pair][1][:, c * P : (c + 1) * P],
+                    rhs=h[hb, half][0][:].bitcast(FP8X4),
+                    rhs_scale=h[hb, half][1][:],
+                    start=(hb == 0 and c == 0),
+                    stop=(hb == PASSES - 1 and c == 1),
+                )
+
+        out_rows = out.rearrange("(c p) j -> p c j", p=P)
+
+        def finish(half, pair):
+            if True:
+                result = tile("result_%d_%d" % (half, pair), [P, 2, HALF], F32)
+                for c in range(2):
+                    bias = out_bias[:, 2 * pair + c : 2 * pair + c + 1]
+                    sums = y[half, pair][:, c * HALF : (c + 1) * HALF]
+                    if half == 0:
+                        nc.scalar.activation(result[:, c, :], sums, ACT.Identity, bias=bias)
+                    else:
+                        nc.vector.tensor_scalar(result[:, c, :], sums, bias, None, ALU.add)
+                nc.sync.dma_start(
+                    out=out_rows[:, 2 * pair : 2 * pair + 2, half * HALF : (half + 1) * HALF], in_=result[:]
+                )
+
+        hidden(1, 0)
+        hidden(1, 1)
+        wo_quantize(0, 0, nc.scalar.copy)
+        wo_quantize(0, 1, nc.vector.tensor_copy)
+        wo_quantize(1, 0, nc.scalar.copy)
+        wo_quantize(1, 1, nc.vector.tensor_copy)
+        for hb in range(PASSES):
+            for pair in range(2):
+                for half in range(2):
+                    y_passes(hb, half, pair)
+        for pair in range(2):
+            for half in range(2):
+                finish(half, pair)

@@ -32,20 +32,20 @@ def tile_list_head_picks_prefix_memory_kernel(
         sb = ctx.enter_context(tc.tile_pool(name="sb", bufs=1))
         psum = ctx.enter_context(tc.psum_pool(name="psum", bufs=1))
 
-        def tile(name, shape, dtype):
-            return sb.tile(shape, dtype, name=name, align_bytes=64)
+        def tile(name, shape, dtype, after=None):
+            return sb.tile(shape, dtype, name=name, tag=after or name, align_bytes=64)
 
         def bank(name, index):
             return psum.tile([P, S], F32, name=name, tag="bank%d" % index)
 
-        def quantize(name, source, columns):
-            codes = tile(name + "_codes", [P, columns], U32)
+        def quantize(name, source, columns, after=None):
+            codes = tile(name + "_codes", [P, columns], U32, after)
             scales = tile(name + "_scales", [P, columns], U8)
             nc.vector.quantize_mx(out=codes[:].bitcast(FP8X4), scales=scales[:], in_=source[:])
             return codes, scales
 
-        def interleave(copy, name, planes, columns):
-            woven = tile(name, [P, PACK * columns], BF16)
+        def interleave(copy, name, planes, columns, after=None):
+            woven = tile(name, [P, PACK * columns], BF16, after)
             copy(
                 out=woven[:].rearrange("p (c j i) -> p c i j", j=4, i=PACK),
                 in_=planes.rearrange("p i (c j) -> p c i j", j=4),
@@ -62,11 +62,6 @@ def tile_list_head_picks_prefix_memory_kernel(
         nc.vector.memset(wm_plane_raw[:].bitcast(I32), 0)
         warm = tile("warm", [P, 1], F32)
         nc.scalar.activation(warm[:], identity[:, 0:1], ACT.Tanh)
-        for q in range(4):
-            nc.gpsimd.dma_start(
-                out=tab_plane[32 * q : 32 * q + 4, :].bitcast(I32).rearrange("r (a c) -> r a c", a=PASSES),
-                in_=tab_scales[:, 4 * q : 4 * q + 4, :].bitcast(I32).rearrange("a r c -> r a c"),
-            )
 
         head_lists = sb.tile([P, S // 16], U16, name="head_lists")
         table_list = sb.tile([P, S // 16], U16, name="table_list")
@@ -88,33 +83,40 @@ def tile_list_head_picks_prefix_memory_kernel(
         load_x(0, 2)
         load_x(0, 3)
         nc.sync.dma_start(table_list[:], offs)
-        for q in range(4):
+
+        def load_scale_rows(plane, scales, q):
             nc.sync.dma_start(
-                out=wm_plane_raw[32 * q : 32 * q + 4, :].bitcast(I32).rearrange("r (a c) -> r a c", a=PASSES),
-                in_=wm_scales[:, 4 * q : 4 * q + 4, :].bitcast(I32).rearrange("a r c -> r a c"),
+                out=plane[32 * q : 32 * q + 4, :].bitcast(I32).rearrange("r (a c) -> r a c", a=PASSES),
+                in_=scales[:, 4 * q : 4 * q + 4, :].bitcast(I32).rearrange("a r c -> r a c"),
             )
+
+        for i in range(PACK):
+            load_x(1, i)
+            load_scale_rows(tab_plane, tab_scales, i)
+            load_scale_rows(wm_plane_raw, wm_scales, i)
         wm_raw = tile("wm_raw", [P, PASSES * 2 * H], U8)
         nc.sync.dma_start(
             out=wm_raw[:].bitcast(I32).rearrange("p (a c) -> p a c", a=PASSES),
             in_=wm_words.bitcast(I32).rearrange("a p c -> p a c"),
         )
         tab = [tile("tab_%d" % a, [P, T], U32) for a in range(PASSES)]
+        wx_rows = wx.rearrange("(a p i) r -> a p i r", a=PASSES, i=PACK)
+        wx_raw = {}
 
         def load_table(a):
             nc.sync.dma_start(
                 out=tab[a][:].bitcast(I32), in_=tab_words[a].rearrange("p t i -> p (t i)").bitcast(I32)
             )
 
-        load_table(0)
-        for i in range(PACK):
-            load_x(1, i)
-        load_table(1)
-        wx_rows = wx.rearrange("(a p i) r -> a p i r", a=PASSES, i=PACK)
-        wx_raw = {}
-        for hb in range(PASSES):
-            for a in range(PASSES):
-                wx_raw[hb, a] = tile("wx_%d_%d" % (hb, a), [P, PACK, PASS], F32)
-                nc.sync.dma_start(out=wx_raw[hb, a][:], in_=wx_rows[a][:, :, hb * PASS : (hb + 1) * PASS])
+        def load_wx(hb, a):
+            wx_raw[hb, a] = tile("wx_%d_%d" % (hb, a), [P, PACK, PASS], F32)
+            nc.sync.dma_start(out=wx_raw[hb, a][:], in_=wx_rows[a][:, :, hb * PASS : (hb + 1) * PASS])
+
+        for a in range(PASSES):
+            load_table(a)
+            load_wx(0, a)
+        for a in range(PASSES):
+            load_wx(1, a)
         wo_rows = wo.rearrange("(b u t s) n -> b t u s n", b=PASSES, t=PACK, s=4)
         wo_raw = []
         for hb in range(PASSES):
@@ -133,11 +135,15 @@ def tile_list_head_picks_prefix_memory_kernel(
             nc.tensor.transpose(turned[:, t * P : (t + 1) * P], rows_ordered[:, t * P : (t + 1) * P], identity[:])
         for c in range(N // P):
             nc.tensor.transpose(turned_bo[:, c * P : (c + 1) * P], rows[:, c * P : (c + 1) * P], identity[:])
-        per_channel = tile("per_channel", [P, 4 * PACK], F32)
-        nc.scalar.copy(
-            out=per_channel[:].rearrange("p (r t) -> p r t", t=PACK),
-            in_=turned[:].rearrange("p (t r) -> p r t", t=PACK)[:, 0:4, :],
-        )
+        bias = {}
+        for hb in range(PASSES):
+            for half in range(2):
+                bias[hb, half] = tile("bias_%d_%d" % (hb, half), [P, PACK], F32)
+                nc.scalar.copy(out=bias[hb, half][:], in_=turned[:, hb:S:P])
+        gain = []
+        for hb in range(PASSES):
+            gain.append(tile("gain_%d" % hb, [P, PACK], F32))
+            nc.scalar.copy(out=gain[hb][:], in_=turned[:, 2 + hb : S : P])
         out_bias = tile("out_bias", [P, N // P], F32)
         nc.scalar.copy(out=out_bias[:], in_=turned_bo[:, 4 : S : P])
 
@@ -149,159 +155,188 @@ def tile_list_head_picks_prefix_memory_kernel(
                 )
             return interleave(nc.scalar.copy, "xg_bf16_%d" % a, picked[:], S)
 
-        xg_bf16 = [gather_x(0)]
+        xg_bf16 = [gather_x(a) for a in range(PASSES)]
 
-        v_scales = []
-        for a in range(PASSES):
-            v_scales.append(tile("v_scales_%d" % a, [P, S], U8))
+        v_scales, v_codes = {}, {}
+
+        def gather_scales(a, after):
+            v_scales[a] = tile("v_scales_%d" % a, [P, S], U8, after)
             nc.vector.tensor_copy(v_scales[a][:], tab_plane[:, a * T : (a + 1) * T].indirect(table_list[:]))
+
+        def gather_codes(a, after):
+            v_codes[a] = tile("v_codes_%d" % a, [P, S], U32, after)
+            nc.vector.tensor_copy(v_codes[a][:], tab[a][:].indirect(table_list[:]))
+
+        gather_scales(0, "x_1_3")
         wm_plane = tile("wm_plane", [P, PASSES * H], U8)
         nc.vector.tensor_copy(
             out=wm_plane[:].bitcast(I32).rearrange("p (e t u) -> p e u t", t=PACK, u=32),
             in_=wm_plane_raw[:].bitcast(I32).rearrange("p (e u t) -> p e u t", t=PACK, u=32),
         )
-        wm_codes = tile("wm_codes", [P, PASSES * 2 * H], U8)
+        wm_codes = tile("wm_codes", [P, PASSES * 2 * H], U8, "weights")
         nc.vector.tensor_copy(
             out=wm_codes[:].bitcast(I32).rearrange("p (e t u w) -> p e u t w", t=PACK, u=32, w=2),
             in_=wm_raw[:].bitcast(I32).rearrange("p (e u t w) -> p e u t w", t=PACK, u=32, w=2),
         )
+        gather_codes(0, "wm_raw")
+        xg = [quantize("xg_0", xg_bf16[0], S, "tab_0")]
 
         z = {}
         for hb in range(PASSES):
             for t in range(PACK):
                 z[hb, t] = bank("z_%d_%d" % (hb, t), PACK * hb + t)
 
-        def table_passes(a):
-            v_codes = tile("v_codes_%d" % a, [P, S], U32)
-            nc.vector.tensor_copy(v_codes[:], tab[a][:].indirect(table_list[:]))
-            for hb in range(PASSES):
-                for t in range(PACK):
-                    c0 = a * H + hb * PASS + t * P
-                    nc.tensor.matmul_mx(
-                        out=z[hb, t][:],
-                        lhsT=wm_codes[:, 2 * c0 : 2 * (c0 + P)].bitcast(FP4X4),
-                        lhsT_scale=wm_plane[:, c0 : c0 + P],
-                        rhs=v_codes[:].bitcast(FP8X4),
-                        rhs_scale=v_scales[a][:],
-                        start=(a == 0),
-                        stop=False,
-                    )
-
-        table_passes(0)
-        xg = [quantize("xg_0", xg_bf16[0], S)]
-        xg_bf16.append(gather_x(1))
-        table_passes(1)
-        xg.append(quantize("xg_1", xg_bf16[1], S))
-
-        def wx_passes(hb, a, copies):
-            woven = []
-            for pair, copy in enumerate(copies):
-                woven.append(tile("wx_bf16_%d_%d_%d" % (hb, a, pair), [P, 2 * PACK * P], BF16))
-                copy(
-                    out=woven[pair][:].rearrange("p (t u s i) -> p u t i s", t=2, s=4, i=PACK),
-                    in_=wx_raw[hb, a][:].rearrange("p i (u t s) -> p u t i s", t=PACK, s=4)[
-                        :, :, 2 * pair : 2 * pair + 2
-                    ],
-                )
-            for pair in range(2):
-                codes, scales = quantize("wx_%d_%d_%d" % (hb, a, pair), woven[pair], 2 * P)
-                for c in range(2):
-                    nc.tensor.matmul_mx(
-                        out=z[hb, 2 * pair + c][:],
-                        lhsT=codes[:, c * P : (c + 1) * P].bitcast(FP8X4),
-                        lhsT_scale=scales[:, c * P : (c + 1) * P],
-                        rhs=xg[a][0][:].bitcast(FP8X4),
-                        rhs_scale=xg[a][1][:],
-                        start=False,
-                        stop=(a == PASSES - 1),
-                    )
-
-        h = {}
-
-        tanh = {}
-
-        def activate(hb, half):
-            cols = slice(half * HALF, (half + 1) * HALF)
-            th = tile("tanh_%d_%d" % (hb, half), [P, PACK, HALF], F32)
+        def table_passes(hb, a):
             for t in range(PACK):
-                nc.scalar.activation(
-                    th[:, t, :], z[hb, t][:, cols], ACT.Tanh, bias=per_channel[:, PACK * hb + t : PACK * hb + t + 1]
+                c0 = a * H + hb * PASS + t * P
+                nc.tensor.matmul_mx(
+                    out=z[hb, t][:],
+                    lhsT=wm_codes[:, 2 * c0 : 2 * (c0 + P)].bitcast(FP4X4),
+                    lhsT_scale=wm_plane[:, c0 : c0 + P],
+                    rhs=v_codes[a][:].bitcast(FP8X4),
+                    rhs_scale=v_scales[a][:],
+                    start=(a == 0),
+                    stop=False,
                 )
-            tanh[hb, half] = th
 
-        def hidden(hb, half):
-            th = tanh[hb, half]
-            gain = per_channel[:, PACK * (2 + hb) : PACK * (3 + hb)]
-            woven = tile("h_bf16_%d_%d" % (hb, half), [P, PACK * HALF], BF16)
-            nc.vector.tensor_tensor(
-                woven[:].rearrange("p (c j t) -> p c t j", j=4, t=PACK),
-                th[:].rearrange("p t (c j) -> p c t j", j=4),
-                gain.rearrange("p (c t j) -> p c t j", c=1, j=1).to_broadcast([P, HALF // 4, PACK, 4]),
-                ALU.mult,
+        wx_bf16 = {}
+
+        def wx_round(hb, a, pair, copy, after):
+            wx_bf16[hb, a, pair] = tile("wx_bf16_%d_%d_%d" % (hb, a, pair), [P, 2 * PACK * P], BF16, after)
+            copy(
+                out=wx_bf16[hb, a, pair][:].rearrange("p (t u s i) -> p u t i s", t=2, s=4, i=PACK),
+                in_=wx_raw[hb, a][:].rearrange("p i (u t s) -> p u t i s", t=PACK, s=4)[:, :, 2 * pair : 2 * pair + 2],
             )
-            h[hb, half] = quantize("h_%d_%d" % (hb, half), woven, HALF)
 
-        shared = (nc.vector.tensor_copy, nc.scalar.copy)
-        wx_passes(0, 0, shared)
-        wx_passes(0, 1, shared)
-        wx_passes(1, 0, (nc.vector.tensor_copy, nc.vector.tensor_copy))
-        activate(0, 0)
-        activate(0, 1)
-        wx_passes(1, 1, shared)
-        hidden(0, 0)
-        activate(1, 0)
-        activate(1, 1)
-        hidden(0, 1)
-
-        wo_q = {}
-        y = {}
-        for half in range(2):
-            for pair in range(2):
-                y[half, pair] = bank("y_%d_%d" % (half, pair), 2 * half + pair)
-
-        def wo_quantize(hb, pair, copy):
-            planes = wo_raw[hb][:, :, 2 * P * pair : 2 * P * (pair + 1)]
-            name = "wo_%d_%d" % (hb, pair)
-            wo_q[hb, pair] = quantize(name, interleave(copy, name + "_bf16", planes, 2 * P), 2 * P)
-
-        def y_passes(hb, half, pair):
+        def wx_passes(hb, a, pair):
+            codes, scales = quantize("wx_%d_%d_%d" % (hb, a, pair), wx_bf16[hb, a, pair], 2 * P)
             for c in range(2):
                 nc.tensor.matmul_mx(
-                    out=y[half, pair][:, c * HALF : (c + 1) * HALF],
-                    lhsT=wo_q[hb, pair][0][:, c * P : (c + 1) * P].bitcast(FP8X4),
-                    lhsT_scale=wo_q[hb, pair][1][:, c * P : (c + 1) * P],
-                    rhs=h[hb, half][0][:].bitcast(FP8X4),
-                    rhs_scale=h[hb, half][1][:],
-                    start=(hb == 0 and c == 0),
-                    stop=(hb == PASSES - 1 and c == 1),
+                    out=z[hb, 2 * pair + c][:],
+                    lhsT=codes[:, c * P : (c + 1) * P].bitcast(FP8X4),
+                    lhsT_scale=scales[:, c * P : (c + 1) * P],
+                    rhs=xg[a][0][:].bitcast(FP8X4),
+                    rhs_scale=xg[a][1][:],
+                    start=False,
+                    stop=(a == PASSES - 1),
                 )
+
+        tanh, h_bf16, h = {}, {}, {}
+
+        def activate(hb, half):
+            tanh[hb, half] = tile("tanh_%d_%d" % (hb, half), [P, PACK, HALF], F32)
+            for t in range(PACK):
+                nc.scalar.activation(
+                    tanh[hb, half][:, t, :],
+                    z[hb, t][:, half * HALF : (half + 1) * HALF],
+                    ACT.Tanh,
+                    bias=bias[hb, half][:, t : t + 1],
+                )
+
+        def h_round(hb, half, after=None):
+            h_bf16[hb, half] = tile("h_bf16_%d_%d" % (hb, half), [P, PACK * HALF], BF16, after)
+            nc.vector.tensor_tensor(
+                h_bf16[hb, half][:].rearrange("p (c j t) -> p c t j", j=4, t=PACK),
+                tanh[hb, half][:].rearrange("p t (c j) -> p c t j", j=4),
+                gain[hb][:].rearrange("p (c t j) -> p c t j", c=1, j=1).to_broadcast([P, HALF // 4, PACK, 4]),
+                ALU.mult,
+            )
+
+        def h_quantize(hb, half):
+            h[hb, half] = quantize("h_%d_%d" % (hb, half), h_bf16[hb, half], HALF)
+
+        wo_bf16, wo_q, y = {}, {}, {}
+
+        def wo_round(hb, pair, copy, after):
+            planes = wo_raw[hb][:, :, 2 * P * pair : 2 * P * (pair + 1)]
+            wo_bf16[hb, pair] = interleave(copy, "wo_bf16_%d_%d" % (hb, pair), planes, 2 * P, after)
+
+        def wo_quantize(hb, pair):
+            wo_q[hb, pair] = quantize("wo_%d_%d" % (hb, pair), wo_bf16[hb, pair], 2 * P)
+
+        def wo_passes(hb, pair):
+            codes, scales = wo_q[hb, pair]
+            for half in range(2):
+                if hb == 0:
+                    y[half, pair] = bank("y_%d_%d" % (half, pair), 2 * half + pair)
+                for c in range(2):
+                    nc.tensor.matmul_mx(
+                        out=y[half, pair][:, c * HALF : (c + 1) * HALF],
+                        lhsT=codes[:, c * P : (c + 1) * P].bitcast(FP8X4),
+                        lhsT_scale=scales[:, c * P : (c + 1) * P],
+                        rhs=h[hb, half][0][:].bitcast(FP8X4),
+                        rhs_scale=h[hb, half][1][:],
+                        start=(hb == 0 and c == 0),
+                        stop=(hb == PASSES - 1 and c == 1),
+                    )
 
         out_rows = out.rearrange("(c p) j -> p c j", p=P)
 
         def finish(half, pair):
-            if True:
-                result = tile("result_%d_%d" % (half, pair), [P, 2, HALF], F32)
-                for c in range(2):
-                    bias = out_bias[:, 2 * pair + c : 2 * pair + c + 1]
-                    sums = y[half, pair][:, c * HALF : (c + 1) * HALF]
-                    if half == 0:
-                        nc.scalar.activation(result[:, c, :], sums, ACT.Identity, bias=bias)
-                    else:
-                        nc.vector.tensor_scalar(result[:, c, :], sums, bias, None, ALU.add)
-                nc.sync.dma_start(
-                    out=out_rows[:, 2 * pair : 2 * pair + 2, half * HALF : (half + 1) * HALF], in_=result[:]
-                )
+            result = tile("result_%d_%d" % (half, pair), [P, 2, HALF], F32)
+            for c in range(2):
+                column = out_bias[:, 2 * pair + c : 2 * pair + c + 1]
+                sums = y[half, pair][:, c * HALF : (c + 1) * HALF]
+                if half == 0:
+                    nc.scalar.activation(result[:, c, :], sums, ACT.Identity, bias=column)
+                else:
+                    nc.vector.tensor_scalar(result[:, c, :], sums, column, None, ALU.add)
+            nc.sync.dma_start(
+                out=out_rows[:, 2 * pair : 2 * pair + 2, half * HALF : (half + 1) * HALF], in_=result[:]
+            )
 
-        hidden(1, 0)
-        hidden(1, 1)
-        wo_quantize(0, 0, nc.scalar.copy)
-        wo_quantize(0, 1, nc.vector.tensor_copy)
-        wo_quantize(1, 0, nc.scalar.copy)
-        wo_quantize(1, 1, nc.vector.tensor_copy)
-        for hb in range(PASSES):
-            for pair in range(2):
-                for half in range(2):
-                    y_passes(hb, half, pair)
+        on_vector, on_scalar = nc.vector.tensor_copy, nc.scalar.copy
+        table_passes(0, 0)
+        table_passes(1, 0)
+        xg.append(quantize("xg_1", xg_bf16[1], S))
+        gather_scales(1, "xg_bf16_0")
+        wx_round(0, 0, 0, on_scalar, "picked_1")
+        wx_round(0, 0, 1, on_scalar, "picked_0")
+        wx_passes(0, 0, 0)
+        gather_codes(1, "xg_bf16_1")
+        table_passes(0, 1)
+        wx_passes(0, 0, 1)
+
+        wx_round(0, 1, 0, on_vector, "picked_0")
+        wx_round(0, 1, 1, on_scalar, "picked_1")
+        wx_passes(0, 1, 0)
+        wx_passes(0, 1, 1)
+        activate(0, 0)
+        activate(0, 1)
+
+        wx_round(1, 0, 0, on_vector, "picked_1")
+        wx_round(1, 0, 1, on_vector, "picked_0")
+        wx_passes(1, 0, 0)
+        wx_passes(1, 0, 1)
+        table_passes(1, 1)
+        h_round(0, 0)
+
+        wx_round(1, 1, 0, on_vector, "tanh_0_0")
+        wx_round(1, 1, 1, on_scalar, "bias_0_1")
+        h_quantize(0, 0)
+        wx_passes(1, 1, 0)
+        wx_passes(1, 1, 1)
+        activate(1, 0)
+        activate(1, 1)
+
+        h_round(0, 1, "bias_0_1")
+        wo_round(0, 0, on_vector, "tanh_0_1")
+        h_quantize(0, 1)
+        h_round(1, 0)
+        wo_quantize(0, 0)
+        wo_passes(0, 0)
+        h_quantize(1, 0)
+        wo_round(1, 0, on_vector, "h_bf16_1_0")
+        wo_round(0, 1, on_scalar, "bias_1_1")
+        wo_round(1, 1, on_scalar, "bias_1_0")
+        h_round(1, 1)
+        wo_quantize(1, 0)
+        h_quantize(1, 1)
+        wo_passes(1, 0)
+        wo_quantize(0, 1)
+        wo_quantize(1, 1)
+        wo_passes(0, 1)
+        wo_passes(1, 1)
         for pair in range(2):
             for half in range(2):
                 finish(half, pair)

@@ -52,14 +52,26 @@ def tile_list_head_picks_prefix_memory_kernel(
             )
             return woven
 
-        tab_plane = tile("tab_plane", [P, PASSES * T], U8)
+        tab_plane = tile("tab_plane", [P, T], U8)
+        v_scales_1 = tile("v_scales_1", [P, S], U8)
         wm_plane_raw = tile("wm_plane_raw", [P, PASSES * H], U8)
         rows = tile("rows", [P, PASS], F32)
         identity = tile("identity", [P, P], F32)
         make_identity(nc, identity[:])
-        nc.vector.memset(rows[:], 0.0)
         nc.vector.memset(tab_plane[:].bitcast(I32), 0)
         nc.vector.memset(wm_plane_raw[:].bitcast(I32), 0)
+        nc.vector.memset(rows[:], 0.0)
+        nc.vector.memset(v_scales_1[:].bitcast(I32), 0)
+        for q in range(4):
+            nc.gpsimd.dma_start(
+                out=tab_plane[32 * q : 32 * q + 8, :].bitcast(I32),
+                in_=tab_scales[:, 4 * q : 4 * q + 4, :].bitcast(I32),
+            )
+        for q in range(4):
+            nc.gpsimd.dma_start(
+                out=wm_plane_raw[32 * q : 32 * q + 4, :].bitcast(I32).rearrange("r (a c) -> r a c", a=PASSES),
+                in_=wm_scales[:, 4 * q : 4 * q + 4, :].bitcast(I32).rearrange("a r c -> r a c"),
+            )
         warm = tile("warm", [P, 1], F32)
         nc.scalar.activation(warm[:], identity[:, 0:1], ACT.Tanh)
 
@@ -83,17 +95,8 @@ def tile_list_head_picks_prefix_memory_kernel(
         load_x(0, 2)
         load_x(0, 3)
         nc.sync.dma_start(table_list[:], offs)
-
-        def load_scale_rows(plane, scales, q):
-            nc.sync.dma_start(
-                out=plane[32 * q : 32 * q + 4, :].bitcast(I32).rearrange("r (a c) -> r a c", a=PASSES),
-                in_=scales[:, 4 * q : 4 * q + 4, :].bitcast(I32).rearrange("a r c -> r a c"),
-            )
-
         for i in range(PACK):
             load_x(1, i)
-            load_scale_rows(tab_plane, tab_scales, i)
-            load_scale_rows(wm_plane_raw, wm_scales, i)
         wm_raw = tile("wm_raw", [P, PASSES * 2 * H], U8)
         nc.sync.dma_start(
             out=wm_raw[:].bitcast(I32).rearrange("p (a c) -> p a c", a=PASSES),
@@ -157,18 +160,17 @@ def tile_list_head_picks_prefix_memory_kernel(
 
         xg_bf16 = [gather_x(a) for a in range(PASSES)]
 
-        v_scales, v_codes = {}, {}
-
-        def gather_scales(a, after):
-            v_scales[a] = tile("v_scales_%d" % a, [P, S], U8, after)
-            nc.vector.tensor_copy(v_scales[a][:], tab_plane[:, a * T : (a + 1) * T].indirect(table_list[:]))
+        v_codes = {}
 
         def gather_codes(a, after):
             v_codes[a] = tile("v_codes_%d" % a, [P, S], U32, after)
             nc.vector.tensor_copy(v_codes[a][:], tab[a][:].indirect(table_list[:]))
 
-        gather_scales(0, "x_1_3")
-        wm_plane = tile("wm_plane", [P, PASSES * H], U8)
+        v_scales_0 = tile("v_scales_0", [P, S], U8, "x_1_3")
+        nc.vector.tensor_copy(v_scales_0[:], tab_plane[:].indirect(table_list[:]))
+        nc.gpsimd.dma_start(out=v_scales_1[0:100, :].bitcast(I32), in_=v_scales_0[4:104, :].bitcast(I32))
+        v_scales = [v_scales_0, v_scales_1]
+        wm_plane = tile("wm_plane", [P, PASSES * H], U8, "tab_plane")
         nc.vector.tensor_copy(
             out=wm_plane[:].bitcast(I32).rearrange("p (e t u) -> p e u t", t=PACK, u=32),
             in_=wm_plane_raw[:].bitcast(I32).rearrange("p (e u t) -> p e u t", t=PACK, u=32),
@@ -270,26 +272,20 @@ def tile_list_head_picks_prefix_memory_kernel(
                         stop=(hb == PASSES - 1 and c == 1),
                     )
 
-        out_rows = out.rearrange("(c p) j -> p c j", p=P)
-
-        def finish(half, pair):
-            result = tile("result_%d_%d" % (half, pair), [P, 2, HALF], F32)
+        def finish(pair):
             for c in range(2):
-                column = out_bias[:, 2 * pair + c : 2 * pair + c + 1]
-                sums = y[half, pair][:, c * HALF : (c + 1) * HALF]
-                if half == 0:
-                    nc.scalar.activation(result[:, c, :], sums, ACT.Identity, bias=column)
-                else:
-                    nc.vector.tensor_scalar(result[:, c, :], sums, column, None, ALU.add)
-            nc.sync.dma_start(
-                out=out_rows[:, 2 * pair : 2 * pair + 2, half * HALF : (half + 1) * HALF], in_=result[:]
-            )
+                n = 2 * pair + c
+                result = tile("result_%d" % n, [P, S], F32)
+                column = out_bias[:, n : n + 1]
+                cols = slice(c * HALF, (c + 1) * HALF)
+                nc.scalar.activation(result[:, :HALF], y[0, pair][:, cols], ACT.Identity, bias=column)
+                nc.vector.tensor_scalar(result[:, HALF:], y[1, pair][:, cols], column, None, ALU.add)
+                nc.sync.dma_start(out=out[n * P : (n + 1) * P, :], in_=result[:])
 
         on_vector, on_scalar = nc.vector.tensor_copy, nc.scalar.copy
         table_passes(0, 0)
         table_passes(1, 0)
         xg.append(quantize("xg_1", xg_bf16[1], S))
-        gather_scales(1, "xg_bf16_0")
         wx_round(0, 0, 0, on_scalar, "picked_1")
         wx_round(0, 0, 1, on_scalar, "picked_0")
         wx_passes(0, 0, 0)
@@ -338,5 +334,4 @@ def tile_list_head_picks_prefix_memory_kernel(
         wo_passes(0, 1)
         wo_passes(1, 1)
         for pair in range(2):
-            for half in range(2):
-                finish(half, pair)
+            finish(pair)

@@ -138,13 +138,10 @@ def tile_list_head_picks_prefix_memory_kernel(
             nc.tensor.transpose(turned[:, t * P : (t + 1) * P], rows_ordered[:, t * P : (t + 1) * P], identity[:])
         for c in range(N // P):
             nc.tensor.transpose(turned_bo[:, c * P : (c + 1) * P], rows[:, c * P : (c + 1) * P], identity[:])
-        bias = {}
+        bias, gain = [], []
         for hb in range(PASSES):
-            for half in range(2):
-                bias[hb, half] = tile("bias_%d_%d" % (hb, half), [P, PACK], F32)
-                nc.scalar.copy(out=bias[hb, half][:], in_=turned[:, hb:S:P])
-        gain = []
-        for hb in range(PASSES):
+            bias.append(tile("bias_%d" % hb, [P, PACK], F32))
+            nc.scalar.copy(out=bias[hb][:], in_=turned[:, hb:S:P])
             gain.append(tile("gain_%d" % hb, [P, PACK], F32))
             nc.scalar.copy(out=gain[hb][:], in_=turned[:, 2 + hb : S : P])
         out_bias = tile("out_bias", [P, N // P], F32)
@@ -223,7 +220,7 @@ def tile_list_head_picks_prefix_memory_kernel(
                     stop=(a == PASSES - 1),
                 )
 
-        tanh, h_bf16, h = {}, {}, {}
+        tanh, h_planes, h_bf16, h = {}, {}, {}, {}
 
         def activate(hb, half):
             tanh[hb, half] = tile("tanh_%d_%d" % (hb, half), [P, PACK, HALF], F32)
@@ -232,17 +229,21 @@ def tile_list_head_picks_prefix_memory_kernel(
                     tanh[hb, half][:, t, :],
                     z[hb, t][:, half * HALF : (half + 1) * HALF],
                     ACT.Tanh,
-                    bias=bias[hb, half][:, t : t + 1],
+                    bias=bias[hb][:, t : t + 1],
                 )
 
         def h_round(hb, half, after=None):
-            h_bf16[hb, half] = tile("h_bf16_%d_%d" % (hb, half), [P, PACK * HALF], BF16, after)
-            nc.vector.tensor_tensor(
-                h_bf16[hb, half][:].rearrange("p (c j t) -> p c t j", j=4, t=PACK),
-                tanh[hb, half][:].rearrange("p t (c j) -> p c t j", j=4),
-                gain[hb][:].rearrange("p (c t j) -> p c t j", c=1, j=1).to_broadcast([P, HALF // 4, PACK, 4]),
-                ALU.mult,
-            )
+            h_planes[hb, half] = tile("h_planes_%d_%d" % (hb, half), [P, PACK, HALF], BF16, after)
+            for t in range(PACK):
+                plane, values, column = h_planes[hb, half][:, t, :], tanh[hb, half][:, t, :], gain[hb][:, t : t + 1]
+                if half == 0:
+                    nc.vector.tensor_scalar(plane, values, column, None, ALU.mult)
+                else:
+                    nc.scalar.activation(plane, values, ACT.Copy, scale=column)
+
+        def h_weave(hb, half, after=None):
+            name = "h_bf16_%d_%d" % (hb, half)
+            h_bf16[hb, half] = interleave(nc.vector.tensor_copy, name, h_planes[hb, half][:], HALF, after)
 
         def h_quantize(hb, half):
             h[hb, half] = quantize("h_%d_%d" % (hb, half), h_bf16[hb, half], HALF)
@@ -305,27 +306,31 @@ def tile_list_head_picks_prefix_memory_kernel(
         wx_passes(1, 0, 0)
         wx_passes(1, 0, 1)
         table_passes(1, 1)
-        h_round(0, 0)
 
-        wx_round(1, 1, 0, on_vector, "tanh_0_0")
-        wx_round(1, 1, 1, on_scalar, "bias_0_1")
-        h_quantize(0, 0)
+        wx_round(1, 1, 0, on_vector, "picked_0")
+        wx_round(1, 1, 1, on_scalar, "bias_0")
+        h_round(0, 0)
+        h_round(0, 1, "wx_1_1")
         wx_passes(1, 1, 0)
         wx_passes(1, 1, 1)
         activate(1, 0)
         activate(1, 1)
 
-        h_round(0, 1, "bias_0_1")
-        wo_round(0, 0, on_vector, "tanh_0_1")
+        h_weave(0, 0, "bias_0")
+        h_weave(0, 1)
+        h_quantize(0, 0)
         h_quantize(0, 1)
+        wo_round(0, 0, on_vector, "h_bf16_0_1")
         h_round(1, 0)
+        h_round(1, 1)
         wo_quantize(0, 0)
         wo_passes(0, 0)
+        h_weave(1, 0)
+        wo_round(1, 0, on_vector, "h_planes_1_0")
+        wo_round(0, 1, on_scalar, "tanh_1_1")
+        wo_round(1, 1, on_scalar, "bias_1")
         h_quantize(1, 0)
-        wo_round(1, 0, on_vector, "h_bf16_1_0")
-        wo_round(0, 1, on_scalar, "bias_1_1")
-        wo_round(1, 1, on_scalar, "bias_1_0")
-        h_round(1, 1)
+        h_weave(1, 1)
         wo_quantize(1, 0)
         h_quantize(1, 1)
         wo_passes(1, 0)

@@ -72,8 +72,6 @@ def tile_list_head_picks_prefix_memory_kernel(
                 out=wm_plane_raw[32 * q : 32 * q + 4, :].bitcast(I32).rearrange("r (a c) -> r a c", a=PASSES),
                 in_=wm_scales[:, 4 * q : 4 * q + 4, :].bitcast(I32).rearrange("a r c -> r a c"),
             )
-        warm = tile("warm", [P, 1], F32)
-        nc.scalar.activation(warm[:], identity[:, 0:1], ACT.Tanh)
 
         head_lists = sb.tile([P, S // 16], U16, name="head_lists")
         table_list = sb.tile([P, S // 16], U16, name="table_list")

@@ -22,6 +22,7 @@ PACK = 4
 PASS = P * PACK
 PASSES = 2
 HALF = S // 2
+RUN = 4
 
 
 def tile_list_head_picks_prefix_memory_kernel(
@@ -38,73 +39,52 @@ def tile_list_head_picks_prefix_memory_kernel(
         def bank(name, index):
             return psum.tile([P, S], F32, name=name, tag="bank%d" % index)
 
-        def quantize(name, source, columns, after=None):
+        def quantize(name, source, columns, after=None, scales_after=None):
             codes = tile(name + "_codes", [P, columns], U32, after)
-            scales = tile(name + "_scales", [P, columns], U8)
+            scales = tile(name + "_scales", [P, columns], U8, scales_after)
             nc.vector.quantize_mx(out=codes[:].bitcast(FP8X4), scales=scales[:], in_=source[:])
             return codes, scales
 
+        def woven_view(woven):
+            return woven[:].rearrange("p (c j i) -> p c i j", j=RUN, i=PACK)
+
+        def planes_view(planes):
+            return planes.rearrange("p i (c j) -> p c i j", j=RUN)
+
         def interleave(copy, name, planes, columns, after=None):
             woven = tile(name, [P, PACK * columns], BF16, after)
-            copy(
-                out=woven[:].rearrange("p (c j i) -> p c i j", j=4, i=PACK),
-                in_=planes.rearrange("p i (c j) -> p c i j", j=4),
-            )
+            copy(out=woven_view(woven), in_=planes_view(planes))
             return woven
+
+        on_vector, on_scalar = nc.vector.tensor_copy, nc.scalar.copy
 
         tab_plane = tile("tab_plane", [P, T], U8)
         v_scales_1 = tile("v_scales_1", [P, S], U8)
         wm_plane_raw = tile("wm_plane_raw", [P, PASSES * H], U8)
-        rows = tile("rows", [P, PASS], F32)
+        rows = tile("rows", [32, PASS], F32)
+        rows_dealt = tile("rows_dealt", [P, PASS], F32)
         identity = tile("identity", [P, P], F32)
-        make_identity(nc, identity[:])
         nc.vector.memset(tab_plane[:].bitcast(I32), 0)
         nc.vector.memset(wm_plane_raw[:].bitcast(I32), 0)
         nc.vector.memset(rows[:], 0.0)
+        nc.vector.memset(rows_dealt[:], 0.0)
         nc.vector.memset(v_scales_1[:].bitcast(I32), 0)
-        for q in range(4):
-            nc.gpsimd.dma_start(
-                out=tab_plane[32 * q : 32 * q + 8, :].bitcast(I32),
-                in_=tab_scales[:, 4 * q : 4 * q + 4, :].bitcast(I32),
-            )
-        for q in range(4):
-            nc.gpsimd.dma_start(
-                out=wm_plane_raw[32 * q : 32 * q + 4, :].bitcast(I32).rearrange("r (a c) -> r a c", a=PASSES),
-                in_=wm_scales[:, 4 * q : 4 * q + 4, :].bitcast(I32).rearrange("a r c -> r a c"),
-            )
+        make_identity(nc, identity[:])
 
         head_lists = sb.tile([P, S // 16], U16, name="head_lists")
         table_list = sb.tile([P, S // 16], U16, name="table_list")
         weights = tile("weights", [P, S], F32)
         x_rows = xT.rearrange("(a p i) t -> a i p t", a=PASSES, i=PACK)
-        x_planes = {}
+        wx_rows = wx.rearrange("(a p i) r -> a p i r", a=PASSES, i=PACK)
+        wo_rows = wo.rearrange("(b u t s) n -> b t u s n", b=PASSES, t=PACK, s=RUN)
+        x_planes, wx_raw, wo_raw, tab = {}, {}, {}, {}
 
         def load_x(a, i):
             x_planes[a, i] = tile("x_%d_%d" % (a, i), [P, TX], F32)
             nc.sync.dma_start(out=x_planes[a, i][:], in_=x_rows[a, i])
 
-        nc.sync.dma_start(head_lists[:], offs2)
-        load_x(0, 0)
-        nc.sync.dma_start(out=weights[:], in_=wgt)
-        load_x(0, 1)
-        nc.sync.dma_start(out=rows[0:2, :], in_=b.rearrange("(h c) -> h c", h=2))
-        nc.sync.dma_start(out=rows[2:4, :], in_=g.rearrange("(h c) -> h c", h=2))
-        nc.sync.dma_start(out=rows[4:5, :], in_=bo.rearrange("(h c) -> h c", h=1))
-        load_x(0, 2)
-        load_x(0, 3)
-        nc.sync.dma_start(table_list[:], offs)
-        for i in range(PACK):
-            load_x(1, i)
-        wm_raw = tile("wm_raw", [P, PASSES * 2 * H], U8)
-        nc.sync.dma_start(
-            out=wm_raw[:].bitcast(I32).rearrange("p (a c) -> p a c", a=PASSES),
-            in_=wm_words.bitcast(I32).rearrange("a p c -> p a c"),
-        )
-        tab = [tile("tab_%d" % a, [P, T], U32) for a in range(PASSES)]
-        wx_rows = wx.rearrange("(a p i) r -> a p i r", a=PASSES, i=PACK)
-        wx_raw = {}
-
         def load_table(a):
+            tab[a] = tile("tab_%d" % a, [P, T], U32)
             nc.sync.dma_start(
                 out=tab[a][:].bitcast(I32), in_=tab_words[a].rearrange("p t i -> p (t i)").bitcast(I32)
             )
@@ -113,228 +93,279 @@ def tile_list_head_picks_prefix_memory_kernel(
             wx_raw[hb, a] = tile("wx_%d_%d" % (hb, a), [P, PACK, PASS], F32)
             nc.sync.dma_start(out=wx_raw[hb, a][:], in_=wx_rows[a][:, :, hb * PASS : (hb + 1) * PASS])
 
-        for a in range(PASSES):
-            load_table(a)
-            load_wx(0, a)
-        for a in range(PASSES):
-            load_wx(1, a)
-        wo_rows = wo.rearrange("(b u t s) n -> b t u s n", b=PASSES, t=PACK, s=4)
-        wo_raw = []
-        for hb in range(PASSES):
-            wo_raw.append(tile("wo_%d" % hb, [P, PACK, N], F32))
+        def load_wo(hb):
+            wo_raw[hb] = tile("wo_%d" % hb, [P, PACK, N], F32)
             for t in range(PACK):
                 nc.sync.dma_start(out=wo_raw[hb][:, t, :], in_=wo_rows[hb, t])
 
-        rows_ordered = tile("rows_ordered", [P, PASS], F32)
-        nc.scalar.copy(
-            out=rows_ordered[:].rearrange("p (t u s) -> p u t s", t=PACK, s=4),
-            in_=rows[:].rearrange("p (u t s) -> p u t s", t=PACK, s=4),
+        def load_table_scales(queue):
+            for q in range(4):
+                queue.dma_start(
+                    out=tab_plane[32 * q : 32 * q + 8, :].bitcast(I32),
+                    in_=tab_scales[:, 4 * q : 4 * q + 4, :].bitcast(I32),
+                )
+
+        def load_wm_scales(queue):
+            for q in range(4):
+                queue.dma_start(
+                    out=wm_plane_raw[32 * q : 32 * q + 4, :].bitcast(I32).rearrange("r (a c) -> r a c", a=PASSES),
+                    in_=wm_scales[:, 4 * q : 4 * q + 4, :].bitcast(I32).rearrange("a r c -> r a c"),
+                )
+
+        def load_rows(queue):
+            queue.dma_start(out=rows[0:2, :], in_=b.rearrange("(h c) -> h c", h=PASSES))
+            queue.dma_start(out=rows[2:4, :], in_=g.rearrange("(h c) -> h c", h=PASSES))
+            queue.dma_start(out=rows_dealt[32:33, :], in_=bo.rearrange("(h c) -> h c", h=1))
+
+        wm_raw, wm_codes = {}, {}
+
+        def load_wm(hb):
+            wm_raw[hb] = tile("wm_raw_%d" % hb, [P, PASSES, PASS // 2], I32)
+            nc.sync.dma_start(
+                out=wm_raw[hb][:],
+                in_=wm_words.bitcast(I32).rearrange("a p c -> p a c")[:, :, hb * PASS // 2 : (hb + 1) * PASS // 2],
+            )
+
+        def wm_order(hb, after):
+            wm_codes[hb] = tile("wm_codes_%d" % hb, [P, PASSES * 2 * PASS], U8, after)
+            nc.vector.tensor_copy(
+                out=wm_codes[hb][:].bitcast(I32).rearrange("p (a t u w) -> p a u t w", t=PACK, u=32, w=2),
+                in_=wm_raw[hb][:].rearrange("p a (u t w) -> p a u t w", t=PACK, w=2),
+            )
+
+        picked = {}
+
+        def gather_x(a, i, after=None):
+            if i == 0:
+                picked[a] = tile("picked_%d" % a, [P, PACK, S], F32, after)
+            nc.vector.tensor_tensor(
+                picked[a][:, i, :], x_planes[a, i][:].indirect(head_lists[:]), weights[:], ALU.mult
+            )
+
+        nc.sync.dma_start(head_lists[:], offs2)
+        nc.sync.dma_start(out=weights[:], in_=wgt)
+        load_x(0, 0)
+        load_x(0, 1)
+        nc.sync.dma_start(table_list[:], offs)
+        load_x(0, 2)
+        load_table_scales(nc.sync)
+        load_x(0, 3)
+        load_rows(nc.sync)
+        load_wx(0, 0)
+        load_x(1, 0)
+        load_wm_scales(nc.sync)
+        load_x(1, 1)
+        load_x(1, 2)
+        load_x(1, 3)
+        load_wx(0, 1)
+        for i in range(PACK):
+            gather_x(0, i)
+        v_scales_0 = tile("v_scales_0", [P, S], U8, "x_0_2")
+        nc.vector.tensor_copy(v_scales_0[:], tab_plane[:].indirect(table_list[:]))
+        nc.sync.dma_start(out=v_scales_1[0:100, :].bitcast(I32), in_=v_scales_0[4:104, :].bitcast(I32))
+        v_scales = [v_scales_0, v_scales_1]
+        load_wm(0)
+        load_table(0)
+        load_table(1)
+        load_wm(1)
+        load_wx(1, 0)
+        load_wx(1, 1)
+        load_wo(0)
+        load_wo(1)
+
+        nc.scalar.activation(
+            rows_dealt[0:32, :].rearrange("p (t u s) -> p u t s", t=PACK, s=RUN),
+            rows[:].rearrange("p (u t s) -> p u t s", t=PACK, s=RUN),
+            ACT.Identity,
         )
-        turned = bank("turned", 6)
-        turned_bo = bank("turned_bo", 7)
+        turned = bank("turned", 7)
         for t in range(PACK):
-            nc.tensor.transpose(turned[:, t * P : (t + 1) * P], rows_ordered[:, t * P : (t + 1) * P], identity[:])
-        for c in range(N // P):
-            nc.tensor.transpose(turned_bo[:, c * P : (c + 1) * P], rows[:, c * P : (c + 1) * P], identity[:])
-        bias, gain = [], []
+            nc.tensor.transpose(turned[:, t * P : (t + 1) * P], rows_dealt[:, t * P : (t + 1) * P], identity[:])
+        consts = tile("consts", [P, 33, PACK], F32)
+        nc.scalar.copy(out=consts[:], in_=turned[:].rearrange("p (t k) -> p k t", t=PACK)[:, 0:33, :])
+        bias = []
         for hb in range(PASSES):
             bias.append(tile("bias_%d" % hb, [P, PACK], F32))
             nc.scalar.copy(out=bias[hb][:], in_=turned[:, hb:S:P])
-            gain.append(tile("gain_%d" % hb, [P, PACK], F32))
-            nc.scalar.copy(out=gain[hb][:], in_=turned[:, 2 + hb : S : P])
-        out_bias = tile("out_bias", [P, N // P], F32)
-        nc.scalar.copy(out=out_bias[:], in_=turned_bo[:, 4 : S : P])
 
-        def gather_x(a):
-            picked = tile("picked_%d" % a, [P, PACK, S], F32)
-            for i in range(PACK):
-                nc.vector.tensor_tensor(
-                    picked[:, i, :], x_planes[a, i][:].indirect(head_lists[:]), weights[:], ALU.mult
-                )
-            return interleave(nc.scalar.copy, "xg_bf16_%d" % a, picked[:], S)
+        wx_bf16, wx_q, xg_bf16, xg, v_codes, z = {}, {}, {}, {}, {}, {}
 
-        xg_bf16 = [gather_x(a) for a in range(PASSES)]
-
-        v_codes = {}
-
-        def gather_codes(a, after):
-            v_codes[a] = tile("v_codes_%d" % a, [P, S], U32, after)
-            nc.vector.tensor_copy(v_codes[a][:], tab[a][:].indirect(table_list[:]))
-
-        v_scales_0 = tile("v_scales_0", [P, S], U8, "x_1_3")
-        nc.vector.tensor_copy(v_scales_0[:], tab_plane[:].indirect(table_list[:]))
-        nc.gpsimd.dma_start(out=v_scales_1[0:100, :].bitcast(I32), in_=v_scales_0[4:104, :].bitcast(I32))
-        v_scales = [v_scales_0, v_scales_1]
-        wm_plane = tile("wm_plane", [P, PASSES * H], U8, "tab_plane")
-        nc.vector.tensor_copy(
-            out=wm_plane[:].bitcast(I32).rearrange("p (e t u) -> p e u t", t=PACK, u=32),
-            in_=wm_plane_raw[:].bitcast(I32).rearrange("p (e u t) -> p e u t", t=PACK, u=32),
-        )
-        wm_codes = tile("wm_codes", [P, PASSES * 2 * H], U8, "weights")
-        nc.vector.tensor_copy(
-            out=wm_codes[:].bitcast(I32).rearrange("p (e t u w) -> p e u t w", t=PACK, u=32, w=2),
-            in_=wm_raw[:].bitcast(I32).rearrange("p (e u t w) -> p e u t w", t=PACK, u=32, w=2),
-        )
-        gather_codes(0, "wm_raw")
-        xg = [quantize("xg_0", xg_bf16[0], S, "tab_0")]
-
-        z = {}
-        for hb in range(PASSES):
-            for t in range(PACK):
-                z[hb, t] = bank("z_%d_%d" % (hb, t), PACK * hb + t)
-
-        def table_passes(hb, a):
-            for t in range(PACK):
-                c0 = a * H + hb * PASS + t * P
-                nc.tensor.matmul_mx(
-                    out=z[hb, t][:],
-                    lhsT=wm_codes[:, 2 * c0 : 2 * (c0 + P)].bitcast(FP4X4),
-                    lhsT_scale=wm_plane[:, c0 : c0 + P],
-                    rhs=v_codes[a][:].bitcast(FP8X4),
-                    rhs_scale=v_scales[a][:],
-                    start=(a == 0),
-                    stop=False,
-                )
-
-        wx_bf16 = {}
-
-        def wx_round(hb, a, pair, copy, after):
-            wx_bf16[hb, a, pair] = tile("wx_bf16_%d_%d_%d" % (hb, a, pair), [P, 2 * PACK * P], BF16, after)
+        def wx_round(hb, a, first, count, copy, after=None):
+            name = "wx_bf16_%d_%d_%d" % (hb, a, first)
+            wx_bf16[hb, a, first] = tile(name, [P, count * PACK * P], BF16, after), count
             copy(
-                out=wx_bf16[hb, a, pair][:].rearrange("p (t u s i) -> p u t i s", t=2, s=4, i=PACK),
-                in_=wx_raw[hb, a][:].rearrange("p i (u t s) -> p u t i s", t=PACK, s=4)[:, :, 2 * pair : 2 * pair + 2],
+                out=wx_bf16[hb, a, first][0][:].rearrange("p (t u s i) -> p u t i s", t=count, s=RUN, i=PACK),
+                in_=wx_raw[hb, a][:].rearrange("p i (u t s) -> p u t i s", t=PACK, s=RUN)[:, :, first : first + count],
             )
 
-        def wx_passes(hb, a, pair):
-            codes, scales = quantize("wx_%d_%d_%d" % (hb, a, pair), wx_bf16[hb, a, pair], 2 * P)
-            for c in range(2):
+        def wx_quantize(hb, a, first, after=None):
+            woven, count = wx_bf16[hb, a, first]
+            wx_q[hb, a, first] = quantize("wx_%d_%d_%d" % (hb, a, first), woven, count * P, after), count
+
+        def z_bank(hb, t):
+            first = (hb, t) not in z
+            if first:
+                z[hb, t] = bank("z_%d_%d" % (hb, t), PACK * hb + t)
+            return z[hb, t], first
+
+        def wx_passes(hb, a, t0, stop=False):
+            (codes, scales), count = wx_q[hb, a, t0]
+            for c in range(count):
+                acc, first = z_bank(hb, t0 + c)
                 nc.tensor.matmul_mx(
-                    out=z[hb, 2 * pair + c][:],
+                    out=acc[:],
                     lhsT=codes[:, c * P : (c + 1) * P].bitcast(FP8X4),
                     lhsT_scale=scales[:, c * P : (c + 1) * P],
                     rhs=xg[a][0][:].bitcast(FP8X4),
                     rhs_scale=xg[a][1][:],
-                    start=False,
-                    stop=(a == PASSES - 1),
+                    start=first,
+                    stop=stop,
                 )
 
-        tanh, h_planes, h_bf16, h = {}, {}, {}, {}
+        def table_passes(hb, a, stop=False):
+            for t in range(PACK):
+                c0 = a * H + hb * PASS + t * P
+                w0 = a * PASS + t * P
+                acc, first = z_bank(hb, t)
+                nc.tensor.matmul_mx(
+                    out=acc[:],
+                    lhsT=wm_codes[hb][:, 2 * w0 : 2 * (w0 + P)].bitcast(FP4X4),
+                    lhsT_scale=wm_plane[:, c0 : c0 + P],
+                    rhs=v_codes[a][:].bitcast(FP8X4),
+                    rhs_scale=v_scales[a][:],
+                    start=first,
+                    stop=stop,
+                )
 
-        def activate(hb, half):
-            tanh[hb, half] = tile("tanh_%d_%d" % (hb, half), [P, PACK, HALF], F32)
+        def gather_codes(a, after=None):
+            v_codes[a] = tile("v_codes_%d" % a, [P, S], U32, after)
+            nc.vector.tensor_copy(v_codes[a][:], tab[a][:].indirect(table_list[:]))
+
+        tanh, h_bf16, h = {}, {}, {}
+
+        def activate(hb, half, after=None):
+            tanh[hb, half] = tile("tanh_%d_%d" % (hb, half), [P, PACK, HALF], F32, after)
             for t in range(PACK):
                 nc.scalar.activation(
                     tanh[hb, half][:, t, :],
                     z[hb, t][:, half * HALF : (half + 1) * HALF],
                     ACT.Tanh,
-                    bias=bias[hb][:, t : t + 1],
+                    bias=(consts[:, hb] if (hb, half) in ((0, 1), (1, 0)) else bias[hb])[:, t : t + 1],
                 )
 
         def h_round(hb, half, after=None):
-            h_planes[hb, half] = tile("h_planes_%d_%d" % (hb, half), [P, PACK, HALF], BF16, after)
-            for t in range(PACK):
-                plane, values, column = h_planes[hb, half][:, t, :], tanh[hb, half][:, t, :], gain[hb][:, t : t + 1]
-                if half == 0:
-                    nc.vector.tensor_scalar(plane, values, column, None, ALU.mult)
-                else:
-                    nc.scalar.activation(plane, values, ACT.Copy, scale=column)
+            h_bf16[hb, half] = tile("h_bf16_%d_%d" % (hb, half), [P, PACK * HALF], BF16, after)
+            gain = consts[:, PASSES + hb, :].unsqueeze(1).unsqueeze(3).to_broadcast([P, HALF // RUN, PACK, RUN])
+            nc.vector.tensor_tensor(woven_view(h_bf16[hb, half]), planes_view(tanh[hb, half][:]), gain, ALU.mult)
 
-        def h_weave(hb, half, after=None):
-            name = "h_bf16_%d_%d" % (hb, half)
-            h_bf16[hb, half] = interleave(nc.vector.tensor_copy, name, h_planes[hb, half][:], HALF, after)
-
-        def h_quantize(hb, half):
-            h[hb, half] = quantize("h_%d_%d" % (hb, half), h_bf16[hb, half], HALF)
+        def h_quantize(hb, half, after=None):
+            h[hb, half] = quantize("h_%d_%d" % (hb, half), h_bf16[hb, half], HALF, after)
 
         wo_bf16, wo_q, y = {}, {}, {}
 
-        def wo_round(hb, pair, copy, after):
+        def wo_round(hb, pair, copy, after=None):
             planes = wo_raw[hb][:, :, 2 * P * pair : 2 * P * (pair + 1)]
             wo_bf16[hb, pair] = interleave(copy, "wo_bf16_%d_%d" % (hb, pair), planes, 2 * P, after)
 
         def wo_quantize(hb, pair):
             wo_q[hb, pair] = quantize("wo_%d_%d" % (hb, pair), wo_bf16[hb, pair], 2 * P)
 
-        def wo_passes(hb, pair):
+        def wo_passes(hb, half, pair):
             codes, scales = wo_q[hb, pair]
-            for half in range(2):
-                if hb == 0:
-                    y[half, pair] = bank("y_%d_%d" % (half, pair), 2 * half + pair)
-                for c in range(2):
-                    nc.tensor.matmul_mx(
-                        out=y[half, pair][:, c * HALF : (c + 1) * HALF],
-                        lhsT=codes[:, c * P : (c + 1) * P].bitcast(FP8X4),
-                        lhsT_scale=scales[:, c * P : (c + 1) * P],
-                        rhs=h[hb, half][0][:].bitcast(FP8X4),
-                        rhs_scale=h[hb, half][1][:],
-                        start=(hb == 0 and c == 0),
-                        stop=(hb == PASSES - 1 and c == 1),
-                    )
-
-        def finish(pair):
+            if hb == 0:
+                y[half, pair] = bank("y_%d_%d" % (half, pair), 2 * half + pair)
             for c in range(2):
-                n = 2 * pair + c
-                result = tile("result_%d" % n, [P, S], F32)
-                column = out_bias[:, n : n + 1]
-                cols = slice(c * HALF, (c + 1) * HALF)
-                nc.scalar.activation(result[:, :HALF], y[0, pair][:, cols], ACT.Identity, bias=column)
-                nc.vector.tensor_scalar(result[:, HALF:], y[1, pair][:, cols], column, None, ALU.add)
-                nc.sync.dma_start(out=out[n * P : (n + 1) * P, :], in_=result[:])
+                nc.tensor.matmul_mx(
+                    out=y[half, pair][:, c * HALF : (c + 1) * HALF],
+                    lhsT=codes[:, c * P : (c + 1) * P].bitcast(FP8X4),
+                    lhsT_scale=scales[:, c * P : (c + 1) * P],
+                    rhs=h[hb, half][0][:].bitcast(FP8X4),
+                    rhs_scale=h[hb, half][1][:],
+                    start=(hb == 0 and c == 0),
+                    stop=(hb == PASSES - 1 and c == 1),
+                )
 
-        on_vector, on_scalar = nc.vector.tensor_copy, nc.scalar.copy
-        table_passes(0, 0)
-        table_passes(1, 0)
-        xg.append(quantize("xg_1", xg_bf16[1], S))
-        wx_round(0, 0, 0, on_scalar, "picked_1")
-        wx_round(0, 0, 1, on_scalar, "picked_0")
+        out_rows = out.rearrange("(q c p) j -> q p c j", q=2, c=2)
+
+        def finish(half, pair, vector):
+            result = tile("result_%d_%d" % (half, pair), [P, 2, HALF], F32)
+            for c in range(2):
+                column = consts[:, 32, 2 * pair + c : 2 * pair + c + 1]
+                sums = y[half, pair][:, c * HALF : (c + 1) * HALF]
+                if vector:
+                    nc.vector.tensor_scalar(result[:, c, :], sums, column, None, ALU.add)
+                else:
+                    nc.scalar.activation(result[:, c, :], sums, ACT.Identity, bias=column)
+            nc.sync.dma_start(out=out_rows[pair][:, :, half * HALF : (half + 1) * HALF], in_=result[:])
+
+        xg_bf16[0] = interleave(on_scalar, "xg_bf16_0", picked[0][:], S)
+        wx_round(0, 0, 0, 4, on_scalar)
+        gather_x(1, 0, "x_0_3")
+        for i in range(1, PACK):
+            gather_x(1, i)
+        wx_round(0, 1, 0, 4, on_scalar, "picked_0")
+        xg_bf16[1] = interleave(on_scalar, "xg_bf16_1", picked[1][:], S, "wx_0_1")
+        xg[0] = quantize("xg_0", xg_bf16[0], S, "x_1_2", "tab_plane")
+        wx_quantize(0, 0, 0, "x_1_3")
         wx_passes(0, 0, 0)
-        gather_codes(1, "xg_bf16_1")
-        table_passes(0, 1)
-        wx_passes(0, 0, 1)
-
-        wx_round(0, 1, 0, on_vector, "picked_0")
-        wx_round(0, 1, 1, on_scalar, "picked_1")
+        wm_plane = tile("wm_plane", [P, PASSES * H], U8, "xg_bf16_0")
+        nc.vector.tensor_copy(
+            out=wm_plane[:].bitcast(I32).rearrange("p (e t u) -> p e u t", t=PACK, u=32),
+            in_=wm_plane_raw[:].bitcast(I32).rearrange("p (e u t) -> p e u t", t=PACK, u=32),
+        )
+        wm_order(0, "wx_bf16_0_0_0")
+        wx_quantize(0, 1, 0, "wm_plane_raw")
+        gather_codes(0, "wm_raw_0")
+        table_passes(0, 0)
+        xg[1] = quantize("xg_1", xg_bf16[1], S, "picked_0")
         wx_passes(0, 1, 0)
-        wx_passes(0, 1, 1)
+        gather_codes(1, "tab_0")
+        table_passes(0, 1, stop=True)
+        wx_round(1, 0, 2, 2, on_scalar, "x_0_3")
         activate(0, 0)
-        activate(0, 1)
 
-        wx_round(1, 0, 0, on_vector, "picked_1")
-        wx_round(1, 0, 1, on_vector, "picked_0")
-        wx_passes(1, 0, 0)
-        wx_passes(1, 0, 1)
+        wm_order(1, "wx_0_1")
+        table_passes(1, 0)
         table_passes(1, 1)
-
-        wx_round(1, 1, 0, on_vector, "picked_0")
-        wx_round(1, 1, 1, on_scalar, "bias_0")
-        h_round(0, 0)
-        h_round(0, 1, "wx_1_1")
-        wx_passes(1, 1, 0)
-        wx_passes(1, 1, 1)
+        wx_round(1, 0, 0, 2, on_vector, "tab_1")
+        wx_round(1, 1, 2, 2, on_scalar, "bias_0")
+        wx_quantize(1, 0, 2, "wm_raw_1")
+        wx_passes(1, 0, 2)
+        wx_quantize(1, 0, 0)
+        wx_passes(1, 0, 0)
+        wx_round(1, 1, 0, 2, on_vector, "x_0_3")
+        activate(0, 1, "wx_1_1")
+        wx_quantize(1, 1, 0, "tab_1")
+        wx_passes(1, 1, 0, stop=True)
+        wx_quantize(1, 1, 2)
+        wx_passes(1, 1, 2, stop=True)
         activate(1, 0)
         activate(1, 1)
-
-        h_weave(0, 0, "bias_0")
-        h_weave(0, 1)
+        h_round(0, 0, "x_0_3")
+        wo_round(0, 0, on_vector, "bias_0")
         h_quantize(0, 0)
-        h_quantize(0, 1)
-        wo_round(0, 0, on_vector, "h_bf16_0_1")
-        h_round(1, 0)
-        h_round(1, 1)
+        h_round(0, 1, "tanh_0_0")
         wo_quantize(0, 0)
-        wo_passes(0, 0)
-        h_weave(1, 0)
-        wo_round(1, 0, on_vector, "h_planes_1_0")
-        wo_round(0, 1, on_scalar, "tanh_1_1")
-        wo_round(1, 1, on_scalar, "bias_1")
+        wo_passes(0, 0, 0)
+        h_round(1, 0)
+        h_quantize(0, 1)
+        wo_passes(0, 1, 0)
+        wo_round(1, 0, on_scalar, "bias_1")
+        wo_round(0, 1, on_scalar, "tanh_1_0")
+        h_round(1, 1)
         h_quantize(1, 0)
-        h_weave(1, 1)
+        wo_round(1, 1, on_scalar, "tanh_1_1")
         wo_quantize(1, 0)
+        wo_passes(1, 0, 0)
         h_quantize(1, 1)
-        wo_passes(1, 0)
+        wo_passes(1, 1, 0)
         wo_quantize(0, 1)
+        wo_passes(0, 0, 1)
+        wo_passes(0, 1, 1)
+        finish(0, 0, True)
+        finish(1, 0, True)
         wo_quantize(1, 1)
-        wo_passes(0, 1)
-        wo_passes(1, 1)
-        for pair in range(2):
-            finish(pair)
+        wo_passes(1, 0, 1)
+        wo_passes(1, 1, 1)
+        finish(0, 1, False)
+        finish(1, 1, True)

@@ -142,33 +142,33 @@ def tile_list_head_picks_prefix_memory_kernel(
                 picked[a][:, i, :], x_planes[a, i][:].indirect(head_lists[:]), weights[:], ALU.mult
             )
 
+        load_table_scales(nc.gpsimd)
+        load_rows(nc.gpsimd)
+        load_wm_scales(nc.gpsimd)
         nc.sync.dma_start(head_lists[:], offs2)
         nc.sync.dma_start(out=weights[:], in_=wgt)
         load_x(0, 0)
         load_x(0, 1)
         nc.sync.dma_start(table_list[:], offs)
         load_x(0, 2)
-        load_table_scales(nc.sync)
         load_x(0, 3)
-        load_rows(nc.sync)
         load_wx(0, 0)
         load_x(1, 0)
-        load_wm_scales(nc.sync)
         load_x(1, 1)
         load_x(1, 2)
-        load_x(1, 3)
         load_wx(0, 1)
+        load_x(1, 3)
         for i in range(PACK):
             gather_x(0, i)
         v_scales_0 = tile("v_scales_0", [P, S], U8, "x_0_2")
         nc.vector.tensor_copy(v_scales_0[:], tab_plane[:].indirect(table_list[:]))
-        nc.sync.dma_start(out=v_scales_1[0:100, :].bitcast(I32), in_=v_scales_0[4:104, :].bitcast(I32))
+        nc.gpsimd.dma_start(out=v_scales_1[0:100, :].bitcast(I32), in_=v_scales_0[4:104, :].bitcast(I32))
         v_scales = [v_scales_0, v_scales_1]
         load_wm(0)
         load_table(0)
         load_table(1)
-        load_wm(1)
         load_wx(1, 0)
+        load_wm(1)
         load_wx(1, 1)
         load_wo(0)
         load_wo(1)
@@ -250,7 +250,7 @@ def tile_list_head_picks_prefix_memory_kernel(
                     tanh[hb, half][:, t, :],
                     z[hb, t][:, half * HALF : (half + 1) * HALF],
                     ACT.Tanh,
-                    bias=(consts[:, hb] if (hb, half) in ((0, 1), (1, 0)) else bias[hb])[:, t : t + 1],
+                    bias=bias[hb][:, t : t + 1],
                 )
 
         def h_round(hb, half, after=None):
@@ -300,72 +300,72 @@ def tile_list_head_picks_prefix_memory_kernel(
 
         xg_bf16[0] = interleave(on_scalar, "xg_bf16_0", picked[0][:], S)
         wx_round(0, 0, 0, 4, on_scalar)
-        gather_x(1, 0, "x_0_3")
+        gather_x(1, 0, "tab_plane")
         for i in range(1, PACK):
             gather_x(1, i)
-        wx_round(0, 1, 0, 4, on_scalar, "picked_0")
+        wx_round(0, 1, 0, 4, on_scalar, "wx_0_0")
         xg_bf16[1] = interleave(on_scalar, "xg_bf16_1", picked[1][:], S, "wx_0_1")
-        xg[0] = quantize("xg_0", xg_bf16[0], S, "x_1_2", "tab_plane")
+        xg[0] = quantize("xg_0", xg_bf16[0], S, "x_1_2")
         wx_quantize(0, 0, 0, "x_1_3")
         wx_passes(0, 0, 0)
-        wm_plane = tile("wm_plane", [P, PASSES * H], U8, "xg_bf16_0")
+        wx_quantize(0, 1, 0, "xg_bf16_0")
+        wm_plane = tile("wm_plane", [P, PASSES * H], U8, "wx_bf16_0_0_0")
         nc.vector.tensor_copy(
             out=wm_plane[:].bitcast(I32).rearrange("p (e t u) -> p e u t", t=PACK, u=32),
             in_=wm_plane_raw[:].bitcast(I32).rearrange("p (e u t) -> p e u t", t=PACK, u=32),
         )
-        wm_order(0, "wx_bf16_0_0_0")
-        wx_quantize(0, 1, 0, "wm_plane_raw")
-        gather_codes(0, "wm_raw_0")
+        wm_order(0, "wx_0_0")
+        gather_codes(0, "wm_plane_raw")
         table_passes(0, 0)
-        xg[1] = quantize("xg_1", xg_bf16[1], S, "picked_0")
+        xg[1] = quantize("xg_1", xg_bf16[1], S, "wm_raw_0")
         wx_passes(0, 1, 0)
         gather_codes(1, "tab_0")
         table_passes(0, 1, stop=True)
-        wx_round(1, 0, 2, 2, on_scalar, "x_0_3")
         activate(0, 0)
+        activate(0, 1)
 
-        wm_order(1, "wx_0_1")
-        table_passes(1, 0)
-        table_passes(1, 1)
-        wx_round(1, 0, 0, 2, on_vector, "tab_1")
-        wx_round(1, 1, 2, 2, on_scalar, "bias_0")
-        wx_quantize(1, 0, 2, "wm_raw_1")
-        wx_passes(1, 0, 2)
+        wx_round(1, 0, 0, 2, on_vector, "wx_0_1")
+        wx_round(1, 0, 2, 2, on_vector, "tab_1")
         wx_quantize(1, 0, 0)
         wx_passes(1, 0, 0)
-        wx_round(1, 1, 0, 2, on_vector, "x_0_3")
-        activate(0, 1, "wx_1_1")
-        wx_quantize(1, 1, 0, "tab_1")
+        wm_order(1, "wx_1_0")
+        wx_quantize(1, 0, 2)
+        wx_passes(1, 0, 2)
+        table_passes(1, 0)
+        table_passes(1, 1)
+        h_round(0, 0, "wm_raw_1")
+        wx_round(1, 1, 0, 2, on_vector, "tab_1")
+        wx_round(1, 1, 2, 2, on_scalar, "bias_0")
+        h_quantize(0, 0)
+        wx_quantize(1, 1, 0)
         wx_passes(1, 1, 0, stop=True)
         wx_quantize(1, 1, 2)
         wx_passes(1, 1, 2, stop=True)
         activate(1, 0)
         activate(1, 1)
-        h_round(0, 0, "x_0_3")
-        wo_round(0, 0, on_vector, "bias_0")
-        h_quantize(0, 0)
-        h_round(0, 1, "tanh_0_0")
+        h_round(0, 1, "bias_0")
+        wo_round(0, 0, on_vector, "tab_1")
+        h_quantize(0, 1)
+        wo_round(0, 1, on_vector, "tanh_0_1")
         wo_quantize(0, 0)
         wo_passes(0, 0, 0)
-        h_round(1, 0)
-        h_quantize(0, 1)
         wo_passes(0, 1, 0)
-        wo_round(1, 0, on_scalar, "bias_1")
-        wo_round(0, 1, on_scalar, "tanh_1_0")
-        h_round(1, 1)
-        h_quantize(1, 0)
-        wo_round(1, 1, on_scalar, "tanh_1_1")
-        wo_quantize(1, 0)
-        wo_passes(1, 0, 0)
-        h_quantize(1, 1)
-        wo_passes(1, 1, 0)
+        h_round(1, 0, "wo_0")
         wo_quantize(0, 1)
         wo_passes(0, 0, 1)
         wo_passes(0, 1, 1)
-        finish(0, 0, True)
-        finish(1, 0, True)
+        wo_round(1, 0, on_scalar, "bias_1")
+        wo_round(1, 1, on_scalar, "tanh_1_0")
+        h_quantize(1, 0)
+        wo_quantize(1, 0)
+        wo_passes(1, 0, 0)
+        h_round(1, 1, "bias_1")
         wo_quantize(1, 1)
         wo_passes(1, 0, 1)
+        finish(0, 0, False)
+        h_quantize(1, 1)
+        wo_passes(1, 1, 0)
         wo_passes(1, 1, 1)
         finish(0, 1, False)
-        finish(1, 1, True)
+        finish(1, 0, True)
+        finish(1, 1, False)

@@ -23,6 +23,10 @@ PASS = P * PACK
 PASSES = 2
 HALF = S // 2
 RUN = 4
+QUAD = 32
+BO_ROW = P - QUAD - 1
+B_ROW = P - 2 * PASSES
+G_ROW = P - PASSES
 
 
 def tile_list_head_picks_prefix_memory_kernel(
@@ -31,6 +35,7 @@ def tile_list_head_picks_prefix_memory_kernel(
     nc = tc.nc
     with ExitStack() as ctx:
         sb = ctx.enter_context(tc.tile_pool(name="sb", bufs=1))
+        placed = ctx.enter_context(tc.tile_pool(name="placed", bufs=1))
         psum = ctx.enter_context(tc.psum_pool(name="psum", bufs=1))
 
         def tile(name, shape, dtype, after=None):
@@ -39,9 +44,10 @@ def tile_list_head_picks_prefix_memory_kernel(
         def bank(name, index):
             return psum.tile([P, S], F32, name=name, tag="bank%d" % index)
 
-        def quantize(name, source, columns, after=None, scales_after=None):
+        def quantize(name, source, columns, after=None, scales=None):
             codes = tile(name + "_codes", [P, columns], U32, after)
-            scales = tile(name + "_scales", [P, columns], U8, scales_after)
+            if scales is None:
+                scales = tile(name + "_scales", [P, columns], U8)
             nc.vector.quantize_mx(out=codes[:].bitcast(FP8X4), scales=scales[:], in_=source[:])
             return codes, scales
 
@@ -58,16 +64,17 @@ def tile_list_head_picks_prefix_memory_kernel(
 
         on_vector, on_scalar = nc.vector.tensor_copy, nc.scalar.copy
 
-        tab_plane = tile("tab_plane", [P, T], U8)
+        tab_plane = placed.tile([P, T], U8, name="tab_plane", offset=0, align_bytes=64)
         v_scales_1 = tile("v_scales_1", [P, S], U8)
         wm_plane_raw = tile("wm_plane_raw", [P, PASSES * H], U8)
-        rows = tile("rows", [32, PASS], F32)
+        wm_plane = tile("wm_plane", [P, PASSES * H], U8)
+        rows = tile("rows", [P, PASS], F32)
         rows_dealt = tile("rows_dealt", [P, PASS], F32)
         identity = tile("identity", [P, P], F32)
         nc.vector.memset(tab_plane[:].bitcast(I32), 0)
-        nc.vector.memset(wm_plane_raw[:].bitcast(I32), 0)
-        nc.vector.memset(rows[:], 0.0)
-        nc.vector.memset(rows_dealt[:], 0.0)
+        nc.vector.memset(wm_plane[:].bitcast(I32), 0)
+        nc.vector.memset(rows[P - QUAD : B_ROW, :], 0.0)
+        nc.vector.memset(rows_dealt[0:BO_ROW, :], 0.0)
         nc.vector.memset(v_scales_1[:].bitcast(I32), 0)
         make_identity(nc, identity[:])
 
@@ -113,38 +120,37 @@ def tile_list_head_picks_prefix_memory_kernel(
                 )
 
         def load_rows(queue):
-            queue.dma_start(out=rows[0:2, :], in_=b.rearrange("(h c) -> h c", h=PASSES))
-            queue.dma_start(out=rows[2:4, :], in_=g.rearrange("(h c) -> h c", h=PASSES))
-            queue.dma_start(out=rows_dealt[32:33, :], in_=bo.rearrange("(h c) -> h c", h=1))
+            queue.dma_start(out=rows[B_ROW:G_ROW, :], in_=b.rearrange("(h c) -> h c", h=PASSES))
+            queue.dma_start(out=rows[G_ROW:P, :], in_=g.rearrange("(h c) -> h c", h=PASSES))
+            queue.dma_start(out=rows_dealt[BO_ROW : BO_ROW + 1, :], in_=bo.rearrange("(h c) -> h c", h=1))
 
         wm_raw, wm_codes = {}, {}
 
-        def load_wm(hb):
-            wm_raw[hb] = tile("wm_raw_%d" % hb, [P, PASSES, PASS // 2], I32)
-            nc.sync.dma_start(
-                out=wm_raw[hb][:],
-                in_=wm_words.bitcast(I32).rearrange("a p c -> p a c")[:, :, hb * PASS // 2 : (hb + 1) * PASS // 2],
-            )
+        def load_wm():
+            wm_raw[0] = tile("wm_raw", [P, PASSES, H // 2], I32)
+            nc.sync.dma_start(out=wm_raw[0][:], in_=wm_words.bitcast(I32).rearrange("a p c -> p a c"))
 
-        def wm_order(hb, after):
-            wm_codes[hb] = tile("wm_codes_%d" % hb, [P, PASSES * 2 * PASS], U8, after)
-            nc.vector.tensor_copy(
-                out=wm_codes[hb][:].bitcast(I32).rearrange("p (a t u w) -> p a u t w", t=PACK, u=32, w=2),
-                in_=wm_raw[hb][:].rearrange("p a (u t w) -> p a u t w", t=PACK, w=2),
+        def wm_order(hb, codes):
+            wm_codes[hb] = codes
+            nc.scalar.copy(
+                out=wm_codes[hb][:].bitcast(U32).rearrange("p (a t u w) -> p a u t w", t=PACK, u=32, w=2),
+                in_=wm_raw[0][:]
+                .bitcast(U32)[:, :, hb * PASS // 2 : (hb + 1) * PASS // 2]
+                .rearrange("p a (u t w) -> p a u t w", t=PACK, w=2),
             )
 
         picked = {}
 
         def gather_x(a, i, after=None):
             if i == 0:
-                picked[a] = tile("picked_%d" % a, [P, PACK, S], F32, after)
+                picked[a] = placed.tile([P, PACK, S], F32, name="picked_%d" % a, offset=after, align_bytes=64)
             nc.vector.tensor_tensor(
                 picked[a][:, i, :], x_planes[a, i][:].indirect(head_lists[:]), weights[:], ALU.mult
             )
 
         load_table_scales(nc.gpsimd)
-        load_rows(nc.gpsimd)
-        load_wm_scales(nc.gpsimd)
+        load_rows(nc.scalar)
+        load_wm_scales(nc.scalar)
         nc.sync.dma_start(head_lists[:], offs2)
         nc.sync.dma_start(out=weights[:], in_=wgt)
         load_x(0, 0)
@@ -159,34 +165,40 @@ def tile_list_head_picks_prefix_memory_kernel(
         load_wx(0, 1)
         load_x(1, 3)
         for i in range(PACK):
-            gather_x(0, i)
+            gather_x(0, i, 4 * PACK * S)
         v_scales_0 = tile("v_scales_0", [P, S], U8, "x_0_2")
         nc.vector.tensor_copy(v_scales_0[:], tab_plane[:].indirect(table_list[:]))
         nc.gpsimd.dma_start(out=v_scales_1[0:100, :].bitcast(I32), in_=v_scales_0[4:104, :].bitcast(I32))
         v_scales = [v_scales_0, v_scales_1]
-        load_wm(0)
+        load_wm()
         load_table(0)
         load_table(1)
         load_wx(1, 0)
-        load_wm(1)
         load_wx(1, 1)
         load_wo(0)
         load_wo(1)
 
         nc.scalar.activation(
-            rows_dealt[0:32, :].rearrange("p (t u s) -> p u t s", t=PACK, s=RUN),
-            rows[:].rearrange("p (u t s) -> p u t s", t=PACK, s=RUN),
+            rows_dealt[P - QUAD : P, :].rearrange("p (t u s) -> p u t s", t=PACK, s=RUN),
+            rows[P - QUAD : P, :].rearrange("p (u t s) -> p u t s", t=PACK, s=RUN),
             ACT.Identity,
         )
         turned = bank("turned", 7)
         for t in range(PACK):
             nc.tensor.transpose(turned[:, t * P : (t + 1) * P], rows_dealt[:, t * P : (t + 1) * P], identity[:])
         consts = tile("consts", [P, 33, PACK], F32)
-        nc.scalar.copy(out=consts[:], in_=turned[:].rearrange("p (t k) -> p k t", t=PACK)[:, 0:33, :])
-        bias = []
+        nc.scalar.copy(out=consts[:], in_=turned[:].rearrange("p (t k) -> p k t", t=PACK)[:, BO_ROW:P, :])
+        bias = {}
         for hb in range(PASSES):
-            bias.append(tile("bias_%d" % hb, [P, PACK], F32))
-            nc.scalar.copy(out=bias[hb][:], in_=turned[:, hb:S:P])
+            for half in range(2):
+                bias[hb, half] = tile("bias_%d_%d" % (hb, half), [P, PACK], F32)
+                nc.scalar.copy(out=bias[hb, half][:], in_=turned[:, B_ROW + hb : S : P])
+        for q in range(4):
+            live = slice(QUAD * q, QUAD * q + 4)
+            nc.scalar.copy(
+                out=wm_plane[live, :].bitcast(U32).rearrange("p (e t u) -> p e u t", t=PACK, u=QUAD),
+                in_=wm_plane_raw[live, :].bitcast(U32).rearrange("p (e u t) -> p e u t", t=PACK, u=QUAD),
+            )
 
         wx_bf16, wx_q, xg_bf16, xg, v_codes, z = {}, {}, {}, {}, {}, {}
 
@@ -237,8 +249,8 @@ def tile_list_head_picks_prefix_memory_kernel(
                     stop=stop,
                 )
 
-        def gather_codes(a, after=None):
-            v_codes[a] = tile("v_codes_%d" % a, [P, S], U32, after)
+        def gather_codes(a, codes):
+            v_codes[a] = codes
             nc.vector.tensor_copy(v_codes[a][:], tab[a][:].indirect(table_list[:]))
 
         tanh, h_bf16, h = {}, {}, {}
@@ -250,12 +262,12 @@ def tile_list_head_picks_prefix_memory_kernel(
                     tanh[hb, half][:, t, :],
                     z[hb, t][:, half * HALF : (half + 1) * HALF],
                     ACT.Tanh,
-                    bias=bias[hb][:, t : t + 1],
+                    bias=bias[hb, half][:, t : t + 1],
                 )
 
         def h_round(hb, half, after=None):
             h_bf16[hb, half] = tile("h_bf16_%d_%d" % (hb, half), [P, PACK * HALF], BF16, after)
-            gain = consts[:, PASSES + hb, :].unsqueeze(1).unsqueeze(3).to_broadcast([P, HALF // RUN, PACK, RUN])
+            gain = consts[:, G_ROW - BO_ROW + hb, :].unsqueeze(1).unsqueeze(3).to_broadcast([P, HALF // RUN, PACK, RUN])
             nc.vector.tensor_tensor(woven_view(h_bf16[hb, half]), planes_view(tanh[hb, half][:]), gain, ALU.mult)
 
         def h_quantize(hb, half, after=None):
@@ -290,7 +302,7 @@ def tile_list_head_picks_prefix_memory_kernel(
         def finish(half, pair, vector):
             result = tile("result_%d_%d" % (half, pair), [P, 2, HALF], F32)
             for c in range(2):
-                column = consts[:, 32, 2 * pair + c : 2 * pair + c + 1]
+                column = consts[:, 0, 2 * pair + c : 2 * pair + c + 1]
                 sums = y[half, pair][:, c * HALF : (c + 1) * HALF]
                 if vector:
                     nc.vector.tensor_scalar(result[:, c, :], sums, column, None, ALU.add)
@@ -300,42 +312,37 @@ def tile_list_head_picks_prefix_memory_kernel(
 
         xg_bf16[0] = interleave(on_scalar, "xg_bf16_0", picked[0][:], S)
         wx_round(0, 0, 0, 4, on_scalar)
-        gather_x(1, 0, "tab_plane")
+        gather_x(1, 0, 0)
         for i in range(1, PACK):
             gather_x(1, i)
         wx_round(0, 1, 0, 4, on_scalar, "wx_0_0")
-        xg_bf16[1] = interleave(on_scalar, "xg_bf16_1", picked[1][:], S, "wx_0_1")
+        wm_order(0, tile("wm_codes_0", [P, PASSES * 2 * PASS], U8, "wx_0_1"))
+        xg_bf16[1] = interleave(on_scalar, "xg_bf16_1", picked[1][:], S)
+        wm_order(1, placed.tile([P, PASSES * 2 * PASS], U8, name="wm_codes_1", offset=4 * S, align_bytes=64))
         xg[0] = quantize("xg_0", xg_bf16[0], S, "x_1_2")
         wx_quantize(0, 0, 0, "x_1_3")
         wx_passes(0, 0, 0)
         wx_quantize(0, 1, 0, "xg_bf16_0")
-        wm_plane = tile("wm_plane", [P, PASSES * H], U8, "wx_bf16_0_0_0")
-        nc.vector.tensor_copy(
-            out=wm_plane[:].bitcast(I32).rearrange("p (e t u) -> p e u t", t=PACK, u=32),
-            in_=wm_plane_raw[:].bitcast(I32).rearrange("p (e u t) -> p e u t", t=PACK, u=32),
-        )
-        wm_order(0, "wx_0_0")
-        gather_codes(0, "wm_plane_raw")
+        gather_codes(0, tile("v_codes_0", [P, S], U32, "wx_bf16_0_0_0"))
         table_passes(0, 0)
-        xg[1] = quantize("xg_1", xg_bf16[1], S, "wm_raw_0")
+        xg[1] = quantize("xg_1", xg_bf16[1], S, "wx_0_0")
         wx_passes(0, 1, 0)
-        gather_codes(1, "tab_0")
+        gather_codes(1, placed.tile([P, S], U32, name="v_codes_1", offset=0, align_bytes=64))
         table_passes(0, 1, stop=True)
         activate(0, 0)
         activate(0, 1)
 
-        wx_round(1, 0, 0, 2, on_vector, "wx_0_1")
+        wx_round(1, 0, 0, 2, on_vector, "xg_bf16_1")
         wx_round(1, 0, 2, 2, on_vector, "tab_1")
         wx_quantize(1, 0, 0)
         wx_passes(1, 0, 0)
-        wm_order(1, "wx_1_0")
         wx_quantize(1, 0, 2)
         wx_passes(1, 0, 2)
         table_passes(1, 0)
         table_passes(1, 1)
-        h_round(0, 0, "wm_raw_1")
-        wx_round(1, 1, 0, 2, on_vector, "tab_1")
-        wx_round(1, 1, 2, 2, on_scalar, "bias_0")
+        h_round(0, 0, "xg_bf16_1")
+        wx_round(1, 1, 0, 2, on_vector, "bias_0_0")
+        wx_round(1, 1, 2, 2, on_scalar, "bias_0_1")
         h_quantize(0, 0)
         wx_quantize(1, 1, 0)
         wx_passes(1, 1, 0, stop=True)
@@ -343,8 +350,8 @@ def tile_list_head_picks_prefix_memory_kernel(
         wx_passes(1, 1, 2, stop=True)
         activate(1, 0)
         activate(1, 1)
-        h_round(0, 1, "bias_0")
-        wo_round(0, 0, on_vector, "tab_1")
+        h_round(0, 1, "bias_0_1")
+        wo_round(0, 0, on_vector, "bias_0_0")
         h_quantize(0, 1)
         wo_round(0, 1, on_vector, "tanh_0_1")
         wo_quantize(0, 0)
@@ -354,12 +361,12 @@ def tile_list_head_picks_prefix_memory_kernel(
         wo_quantize(0, 1)
         wo_passes(0, 0, 1)
         wo_passes(0, 1, 1)
-        wo_round(1, 0, on_scalar, "bias_1")
+        wo_round(1, 0, on_scalar, "bias_1_1")
         wo_round(1, 1, on_scalar, "tanh_1_0")
         h_quantize(1, 0)
         wo_quantize(1, 0)
         wo_passes(1, 0, 0)
-        h_round(1, 1, "bias_1")
+        h_round(1, 1, "bias_1_1")
         wo_quantize(1, 1)
         wo_passes(1, 0, 1)
         finish(0, 0, False)

@@ -322,13 +322,15 @@ def tile_list_head_picks_prefix_memory_kernel(
         xg[0] = quantize("xg_0", xg_bf16[0], S, "x_1_2")
         wx_quantize(0, 0, 0, "x_1_3")
         wx_passes(0, 0, 0)
-        wx_quantize(0, 1, 0, "xg_bf16_0")
+        wx_quantize(0, 1, 0, "weights")
         gather_codes(0, tile("v_codes_0", [P, S], U32, "wx_bf16_0_0_0"))
         table_passes(0, 0)
-        xg[1] = quantize("xg_1", xg_bf16[1], S, "wx_0_0")
+        xg[1] = quantize("xg_1", xg_bf16[1], S, "tab_0")
         wx_passes(0, 1, 0)
         gather_codes(1, placed.tile([P, S], U32, name="v_codes_1", offset=0, align_bytes=64))
         table_passes(0, 1, stop=True)
+        table_passes(1, 1)
+        table_passes(1, 0)
         activate(0, 0)
         activate(0, 1)
 
@@ -338,8 +340,6 @@ def tile_list_head_picks_prefix_memory_kernel(
         wx_passes(1, 0, 0)
         wx_quantize(1, 0, 2)
         wx_passes(1, 0, 2)
-        table_passes(1, 0)
-        table_passes(1, 1)
         h_round(0, 0, "xg_bf16_1")
         wx_round(1, 1, 0, 2, on_vector, "bias_0_0")
         wx_round(1, 1, 2, 2, on_scalar, "bias_0_1")

@@ -270,6 +270,17 @@ def tile_list_head_picks_prefix_memory_kernel(
             gain = consts[:, G_ROW - BO_ROW + hb, :].unsqueeze(1).unsqueeze(3).to_broadcast([P, HALF // RUN, PACK, RUN])
             nc.vector.tensor_tensor(woven_view(h_bf16[hb, half]), planes_view(tanh[hb, half][:]), gain, ALU.mult)
 
+        def h_scale(hb, half, after):
+            planes = tile("h_planes_%d_%d" % (hb, half), [P, PACK, HALF], BF16, after)
+            for t in range(PACK):
+                nc.scalar.activation(
+                    planes[:, t, :],
+                    tanh[hb, half][:, t, :],
+                    ACT.Identity,
+                    scale=consts[:, G_ROW - BO_ROW + hb, t : t + 1],
+                )
+            return planes
+
         def h_quantize(hb, half, after=None):
             h[hb, half] = quantize("h_%d_%d" % (hb, half), h_bf16[hb, half], HALF, after)
 
@@ -343,6 +354,7 @@ def tile_list_head_picks_prefix_memory_kernel(
         h_round(0, 0, "xg_bf16_1")
         wx_round(1, 1, 0, 2, on_vector, "bias_0_0")
         wx_round(1, 1, 2, 2, on_scalar, "bias_0_1")
+        scaled = h_scale(0, 1, "wx_1_1")
         h_quantize(0, 0)
         wx_quantize(1, 1, 0)
         wx_passes(1, 1, 0, stop=True)
@@ -350,7 +362,7 @@ def tile_list_head_picks_prefix_memory_kernel(
         wx_passes(1, 1, 2, stop=True)
         activate(1, 0)
         activate(1, 1)
-        h_round(0, 1, "bias_0_1")
+        h_bf16[0, 1] = interleave(on_vector, "h_bf16_0_1", scaled[:], HALF, "bias_0_1")
         wo_round(0, 0, on_vector, "bias_0_0")
         h_quantize(0, 1)
         wo_round(0, 1, on_vector, "tanh_0_1")

@@ -290,36 +290,40 @@ def tile_list_head_picks_prefix_memory_kernel(
             planes = wo_raw[hb][:, :, 2 * P * pair : 2 * P * (pair + 1)]
             wo_bf16[hb, pair] = interleave(copy, "wo_bf16_%d_%d" % (hb, pair), planes, 2 * P, after)
 
+        def wo_tile_round(n, copy):
+            woven = wo_bf16[1, 1][:, (n % 2) * PASS : (n % 2 + 1) * PASS]
+            copy(
+                out=woven.rearrange("p (c j i) -> p c i j", j=RUN, i=PACK),
+                in_=planes_view(wo_raw[1][:, :, n * P : (n + 1) * P]),
+            )
+
         def wo_quantize(hb, pair):
             wo_q[hb, pair] = quantize("wo_%d_%d" % (hb, pair), wo_bf16[hb, pair], 2 * P)
 
-        def wo_passes(hb, half, pair):
+        def wo_passes(hb, half, pair, tiles=range(2)):
             codes, scales = wo_q[hb, pair]
-            if hb == 0:
-                y[half, pair] = bank("y_%d_%d" % (half, pair), 2 * half + pair)
-            for c in range(2):
+            for c in tiles:
+                n = 2 * pair + c
+                if hb == 0 and half == 0:
+                    y[n] = bank("y_%d" % n, n)
                 nc.tensor.matmul_mx(
-                    out=y[half, pair][:, c * HALF : (c + 1) * HALF],
+                    out=y[n][:, half * HALF : (half + 1) * HALF],
                     lhsT=codes[:, c * P : (c + 1) * P].bitcast(FP8X4),
                     lhsT_scale=scales[:, c * P : (c + 1) * P],
                     rhs=h[hb, half][0][:].bitcast(FP8X4),
                     rhs_scale=h[hb, half][1][:],
-                    start=(hb == 0 and c == 0),
-                    stop=(hb == PASSES - 1 and c == 1),
+                    start=(hb == 0 and half == 0),
+                    stop=(hb == PASSES - 1 and half == 1),
                 )
 
-        out_rows = out.rearrange("(q c p) j -> q p c j", q=2, c=2)
-
-        def finish(half, pair, vector):
-            result = tile("result_%d_%d" % (half, pair), [P, 2, HALF], F32)
-            for c in range(2):
-                column = consts[:, 0, 2 * pair + c : 2 * pair + c + 1]
-                sums = y[half, pair][:, c * HALF : (c + 1) * HALF]
-                if vector:
-                    nc.vector.tensor_scalar(result[:, c, :], sums, column, None, ALU.add)
-                else:
-                    nc.scalar.activation(result[:, c, :], sums, ACT.Identity, bias=column)
-            nc.sync.dma_start(out=out_rows[pair][:, :, half * HALF : (half + 1) * HALF], in_=result[:])
+        def finish(n, vector):
+            result = tile("result_%d" % n, [P, S], F32)
+            column = consts[:, 0, n : n + 1]
+            if vector:
+                nc.vector.tensor_scalar(result[:], y[n][:], column, None, ALU.add)
+            else:
+                nc.scalar.activation(result[:], y[n][:], ACT.Identity, bias=column)
+            nc.sync.dma_start(out=out[n * P : (n + 1) * P, :], in_=result[:])
 
         xg_bf16[0] = interleave(on_scalar, "xg_bf16_0", picked[0][:], S)
         wx_round(0, 0, 0, 4, on_scalar)
@@ -374,17 +378,18 @@ def tile_list_head_picks_prefix_memory_kernel(
         wo_passes(0, 0, 1)
         wo_passes(0, 1, 1)
         wo_round(1, 0, on_scalar, "bias_1_1")
-        wo_round(1, 1, on_scalar, "tanh_1_0")
+        wo_bf16[1, 1] = tile("wo_bf16_1_1", [P, 2 * PASS], BF16, "tanh_1_0")
+        wo_tile_round(2, on_scalar)
         h_quantize(1, 0)
+        h_round(1, 1)
+        wo_tile_round(3, on_vector)
         wo_quantize(1, 0)
         wo_passes(1, 0, 0)
-        h_round(1, 1, "bias_1_1")
-        wo_quantize(1, 1)
-        wo_passes(1, 0, 1)
-        finish(0, 0, False)
         h_quantize(1, 1)
         wo_passes(1, 1, 0)
-        wo_passes(1, 1, 1)
-        finish(0, 1, False)
-        finish(1, 0, True)
-        finish(1, 1, False)
+        wo_quantize(1, 1)
+        for c in range(2):
+            for half in range(2):
+                wo_passes(1, half, 1, [c])
+        for n in range(PACK):
+            finish(n, n % 2 == 1)

@@ -290,13 +290,6 @@ def tile_list_head_picks_prefix_memory_kernel(
             planes = wo_raw[hb][:, :, 2 * P * pair : 2 * P * (pair + 1)]
             wo_bf16[hb, pair] = interleave(copy, "wo_bf16_%d_%d" % (hb, pair), planes, 2 * P, after)
 
-        def wo_tile_round(n, copy):
-            woven = wo_bf16[1, 1][:, (n % 2) * PASS : (n % 2 + 1) * PASS]
-            copy(
-                out=woven.rearrange("p (c j i) -> p c i j", j=RUN, i=PACK),
-                in_=planes_view(wo_raw[1][:, :, n * P : (n + 1) * P]),
-            )
-
         def wo_quantize(hb, pair):
             wo_q[hb, pair] = quantize("wo_%d_%d" % (hb, pair), wo_bf16[hb, pair], 2 * P)
 
@@ -304,26 +297,32 @@ def tile_list_head_picks_prefix_memory_kernel(
             codes, scales = wo_q[hb, pair]
             for c in tiles:
                 n = 2 * pair + c
-                if hb == 0 and half == 0:
-                    y[n] = bank("y_%d" % n, n)
+                if hb == 0:
+                    y[n, half] = bank("y_%d_%d" % (n, half), PACK * pair + 2 * half + c)
                 nc.tensor.matmul_mx(
-                    out=y[n][:, half * HALF : (half + 1) * HALF],
+                    out=y[n, half][:, 0:HALF],
                     lhsT=codes[:, c * P : (c + 1) * P].bitcast(FP8X4),
                     lhsT_scale=scales[:, c * P : (c + 1) * P],
                     rhs=h[hb, half][0][:].bitcast(FP8X4),
                     rhs_scale=h[hb, half][1][:],
-                    start=(hb == 0 and half == 0),
-                    stop=(hb == PASSES - 1 and half == 1),
+                    start=(hb == 0),
+                    stop=(hb == PASSES - 1),
                 )
 
-        def finish(n, vector):
-            result = tile("result_%d" % n, [P, S], F32)
+        result = {}
+
+        def add_bias(n, half, vector):
+            if n not in result:
+                result[n] = tile("result_%d" % n, [P, S], F32)
+            target = result[n][:, half * HALF : (half + 1) * HALF]
             column = consts[:, 0, n : n + 1]
             if vector:
-                nc.vector.tensor_scalar(result[:], y[n][:], column, None, ALU.add)
+                nc.vector.tensor_scalar(target, y[n, half][:, 0:HALF], column, None, ALU.add)
             else:
-                nc.scalar.activation(result[:], y[n][:], ACT.Identity, bias=column)
-            nc.sync.dma_start(out=out[n * P : (n + 1) * P, :], in_=result[:])
+                nc.scalar.activation(target, y[n, half][:, 0:HALF], ACT.Identity, bias=column)
+
+        def store(n):
+            nc.sync.dma_start(out=out[n * P : (n + 1) * P, :], in_=result[n][:])
 
         xg_bf16[0] = interleave(on_scalar, "xg_bf16_0", picked[0][:], S)
         wx_round(0, 0, 0, 4, on_scalar)
@@ -378,18 +377,24 @@ def tile_list_head_picks_prefix_memory_kernel(
         wo_passes(0, 0, 1)
         wo_passes(0, 1, 1)
         wo_round(1, 0, on_scalar, "bias_1_1")
-        wo_bf16[1, 1] = tile("wo_bf16_1_1", [P, 2 * PASS], BF16, "tanh_1_0")
-        wo_tile_round(2, on_scalar)
+        wo_round(1, 1, on_scalar, "tanh_1_0")
         h_quantize(1, 0)
         h_round(1, 1)
-        wo_tile_round(3, on_vector)
         wo_quantize(1, 0)
         wo_passes(1, 0, 0)
+        add_bias(0, 0, False)
+        add_bias(1, 0, False)
         h_quantize(1, 1)
         wo_passes(1, 1, 0)
         wo_quantize(1, 1)
         for c in range(2):
             for half in range(2):
                 wo_passes(1, half, 1, [c])
-        for n in range(PACK):
-            finish(n, n % 2 == 1)
+        add_bias(0, 1, False)
+        store(0)
+        add_bias(1, 1, True)
+        store(1)
+        for n in range(2, PACK):
+            add_bias(n, 0, False)
+            add_bias(n, 1, True)
+            store(n)

@@ -27,6 +27,7 @@ QUAD = 32
 BO_ROW = P - QUAD - 1
 B_ROW = P - 2 * PASSES
 G_ROW = P - PASSES
+LAST = PACK - 1
 
 
 def tile_list_head_picks_prefix_memory_kernel(
@@ -255,9 +256,10 @@ def tile_list_head_picks_prefix_memory_kernel(
 
         tanh, h_bf16, h = {}, {}, {}
 
-        def activate(hb, half, after=None):
-            tanh[hb, half] = tile("tanh_%d_%d" % (hb, half), [P, PACK, HALF], F32, after)
-            for t in range(PACK):
+        def activate(hb, half, tiles=range(PACK)):
+            if (hb, half) not in tanh:
+                tanh[hb, half] = tile("tanh_%d_%d" % (hb, half), [P, PACK, HALF], F32)
+            for t in tiles:
                 nc.scalar.activation(
                     tanh[hb, half][:, t, :],
                     z[hb, t][:, half * HALF : (half + 1) * HALF],
@@ -290,6 +292,25 @@ def tile_list_head_picks_prefix_memory_kernel(
             planes = wo_raw[hb][:, :, 2 * P * pair : 2 * P * (pair + 1)]
             wo_bf16[hb, pair] = interleave(copy, "wo_bf16_%d_%d" % (hb, pair), planes, 2 * P, after)
 
+        def wo_tile_round(n, copy, after):
+            planes = wo_raw[0][:, :, n * P : (n + 1) * P]
+            wo_bf16[0, n] = interleave(copy, "wo_bf16_tile_%d" % n, planes, P, after)
+
+        def wo_tile_quantize(n):
+            codes, scales = quantize("wo_0_tile_%d" % n, wo_bf16[0, n], P)
+            for half in range(2):
+                if n != LAST:
+                    y[n, half] = bank("y_%d_%d" % (n, half), PACK + 2 * half + n % 2)
+                nc.tensor.matmul_mx(
+                    out=y[n, half][:, 0:HALF],
+                    lhsT=codes[:].bitcast(FP8X4),
+                    lhsT_scale=scales[:],
+                    rhs=h[0, half][0][:].bitcast(FP8X4),
+                    rhs_scale=h[0, half][1][:],
+                    start=(n != LAST),
+                    stop=(n == LAST),
+                )
+
         def wo_quantize(hb, pair):
             wo_q[hb, pair] = quantize("wo_%d_%d" % (hb, pair), wo_bf16[hb, pair], 2 * P)
 
@@ -297,7 +318,7 @@ def tile_list_head_picks_prefix_memory_kernel(
             codes, scales = wo_q[hb, pair]
             for c in tiles:
                 n = 2 * pair + c
-                if hb == 0:
+                if (n, half) not in y:
                     y[n, half] = bank("y_%d_%d" % (n, half), PACK * pair + 2 * half + c)
                 nc.tensor.matmul_mx(
                     out=y[n, half][:, 0:HALF],
@@ -305,8 +326,8 @@ def tile_list_head_picks_prefix_memory_kernel(
                     lhsT_scale=scales[:, c * P : (c + 1) * P],
                     rhs=h[hb, half][0][:].bitcast(FP8X4),
                     rhs_scale=h[hb, half][1][:],
-                    start=(hb == 0),
-                    stop=(hb == PASSES - 1),
+                    start=(hb == 0 or n == LAST),
+                    stop=(hb == 1 and n != LAST),
                 )
 
         result = {}
@@ -368,33 +389,30 @@ def tile_list_head_picks_prefix_memory_kernel(
         h_bf16[0, 1] = interleave(on_vector, "h_bf16_0_1", scaled[:], HALF, "bias_0_1")
         wo_round(0, 0, on_vector, "bias_0_0")
         h_quantize(0, 1)
-        wo_round(0, 1, on_vector, "tanh_0_1")
+        wo_tile_round(2, on_vector, "tanh_0_1")
         wo_quantize(0, 0)
         wo_passes(0, 0, 0)
         wo_passes(0, 1, 0)
-        h_round(1, 0, "wo_0")
-        wo_quantize(0, 1)
-        wo_passes(0, 0, 1)
-        wo_passes(0, 1, 1)
+        h_round(1, 0)
+        wo_tile_quantize(2)
         wo_round(1, 0, on_scalar, "bias_1_1")
         wo_round(1, 1, on_scalar, "tanh_1_0")
         h_quantize(1, 0)
+        wo_tile_round(3, on_scalar, "h_bf16_1_0")
         h_round(1, 1)
         wo_quantize(1, 0)
         wo_passes(1, 0, 0)
-        add_bias(0, 0, False)
-        add_bias(1, 0, False)
         h_quantize(1, 1)
         wo_passes(1, 1, 0)
         wo_quantize(1, 1)
         for c in range(2):
             for half in range(2):
                 wo_passes(1, half, 1, [c])
+        add_bias(0, 0, True)
         add_bias(0, 1, False)
         store(0)
-        add_bias(1, 1, True)
-        store(1)
-        for n in range(2, PACK):
+        wo_tile_quantize(3)
+        for n in range(1, PACK):
             add_bias(n, 0, False)
             add_bias(n, 1, True)
             store(n)

@@ -296,8 +296,8 @@ def tile_list_head_picks_prefix_memory_kernel(
             planes = wo_raw[0][:, :, n * P : (n + 1) * P]
             wo_bf16[0, n] = interleave(copy, "wo_bf16_tile_%d" % n, planes, P, after)
 
-        def wo_tile_quantize(n):
-            codes, scales = quantize("wo_0_tile_%d" % n, wo_bf16[0, n], P)
+        def wo_tile_quantize(n, after=None):
+            codes, scales = quantize("wo_0_tile_%d" % n, wo_bf16[0, n], P, after)
             for half in range(2):
                 if n != LAST:
                     y[n, half] = bank("y_%d_%d" % (n, half), PACK + 2 * half + n % 2)
@@ -311,8 +311,8 @@ def tile_list_head_picks_prefix_memory_kernel(
                     stop=(n == LAST),
                 )
 
-        def wo_quantize(hb, pair):
-            wo_q[hb, pair] = quantize("wo_%d_%d" % (hb, pair), wo_bf16[hb, pair], 2 * P)
+        def wo_quantize(hb, pair, after=None):
+            wo_q[hb, pair] = quantize("wo_%d_%d" % (hb, pair), wo_bf16[hb, pair], 2 * P, after)
 
         def wo_passes(hb, half, pair, tiles=range(2)):
             codes, scales = wo_q[hb, pair]
@@ -390,29 +390,34 @@ def tile_list_head_picks_prefix_memory_kernel(
         wo_round(0, 0, on_vector, "bias_0_0")
         h_quantize(0, 1)
         wo_tile_round(2, on_vector, "tanh_0_1")
-        wo_quantize(0, 0)
+        h_round(1, 0)
+        wo_quantize(0, 0, "bias_1_0")
         wo_passes(0, 0, 0)
         wo_passes(0, 1, 0)
-        h_round(1, 0)
-        wo_tile_quantize(2)
         wo_round(1, 0, on_scalar, "bias_1_1")
         wo_round(1, 1, on_scalar, "tanh_1_0")
         h_quantize(1, 0)
-        wo_tile_round(3, on_scalar, "h_bf16_1_0")
         h_round(1, 1)
         wo_quantize(1, 0)
         wo_passes(1, 0, 0)
         h_quantize(1, 1)
         wo_passes(1, 1, 0)
+        wo_tile_quantize(2, "tanh_1_1")
         wo_quantize(1, 1)
         for c in range(2):
             for half in range(2):
                 wo_passes(1, half, 1, [c])
-        add_bias(0, 0, True)
+        add_bias(0, 0, False)
         add_bias(0, 1, False)
         store(0)
+        wo_tile_round(3, on_scalar, "h_bf16_1_1")
+        add_bias(1, 0, True)
+        add_bias(1, 1, True)
+        store(1)
+        add_bias(2, 0, True)
+        add_bias(2, 1, False)
+        store(2)
         wo_tile_quantize(3)
-        for n in range(1, PACK):
-            add_bias(n, 0, False)
-            add_bias(n, 1, True)
-            store(n)
+        add_bias(3, 0, False)
+        add_bias(3, 1, True)
+        store(3)

@@ -390,6 +390,17 @@ def tile_list_head_picks_prefix_memory_kernel(
         wo_round(0, 0, on_vector, "bias_0_0")
         h_quantize(0, 1)
         wo_tile_round(2, on_vector, "tanh_0_1")
+        for t in range(2):
+            codes, scales = wx_q[1, 1, 2][0]
+            nc.tensor.matmul_mx(
+                out=bank("warm_%d" % t, PACK + t)[:],
+                lhsT=codes[:, t * P : (t + 1) * P].bitcast(FP8X4),
+                lhsT_scale=scales[:, t * P : (t + 1) * P],
+                rhs=xg[1][0][:].bitcast(FP8X4),
+                rhs_scale=xg[1][1][:],
+                start=True,
+                stop=True,
+            )
         h_round(1, 0)
         wo_quantize(0, 0, "bias_1_0")
         wo_passes(0, 0, 0)

@@ -24,6 +24,7 @@ PASSES = 2
 HALF = S // 2
 RUN = 4
 QUAD = 32
+GROUP = 16
 BO_ROW = P - QUAD - 1
 B_ROW = P - 2 * PASSES
 G_ROW = P - PASSES
@@ -82,6 +83,9 @@ def tile_list_head_picks_prefix_memory_kernel(
         head_lists = sb.tile([P, S // 16], U16, name="head_lists")
         table_list = sb.tile([P, S // 16], U16, name="table_list")
         weights = tile("weights", [P, S], F32)
+        weight_pieces = tile("weight_pieces", [P, QUAD], F32)
+        weight_columns = tile("weight_columns", [P, QUAD], F32)
+        weight_spread = tile("weight_spread", [P, S], F32)
         x_rows = xT.rearrange("(a p i) t -> a i p t", a=PASSES, i=PACK)
         wx_rows = wx.rearrange("(a p i) r -> a p i r", a=PASSES, i=PACK)
         wo_rows = wo.rearrange("(b u t s) n -> b t u s n", b=PASSES, t=PACK, s=RUN)
@@ -152,8 +156,8 @@ def tile_list_head_picks_prefix_memory_kernel(
         load_table_scales(nc.gpsimd)
         load_rows(nc.scalar)
         load_wm_scales(nc.scalar)
+        nc.sync.dma_start(out=weight_pieces[:], in_=wgt.rearrange("(g s) (b r) -> g s b r", s=GROUP, r=QUAD)[:, 0])
         nc.sync.dma_start(head_lists[:], offs2)
-        nc.sync.dma_start(out=weights[:], in_=wgt)
         load_x(0, 0)
         load_x(0, 1)
         nc.sync.dma_start(table_list[:], offs)
@@ -165,6 +169,12 @@ def tile_list_head_picks_prefix_memory_kernel(
         load_x(1, 2)
         load_wx(0, 1)
         load_x(1, 3)
+        nc.vector.transpose(weight_columns[:], weight_pieces[:])
+        nc.vector.tensor_copy(
+            out=weight_spread[:].rearrange("p (b h s) -> p b h s", h=2, s=GROUP),
+            in_=weight_columns[:].rearrange("p (h b) -> p b h", h=2).unsqueeze(3).to_broadcast([P, S // QUAD, 2, GROUP]),
+        )
+        nc.vector.transpose(weights[:], weight_spread[:])
         for i in range(PACK):
             gather_x(0, i, 4 * PACK * S)
         v_scales_0 = tile("v_scales_0", [P, S], U8, "x_0_2")

@@ -29,6 +29,7 @@ BO_ROW = P - QUAD - 1
 B_ROW = P - 2 * PASSES
 G_ROW = P - PASSES
 LAST = PACK - 1
+LAST_PLANE = 2 * 4 * PACK * S
 
 
 def tile_list_head_picks_prefix_memory_kernel(
@@ -41,6 +42,8 @@ def tile_list_head_picks_prefix_memory_kernel(
         psum = ctx.enter_context(tc.psum_pool(name="psum", bufs=1))
 
         def tile(name, shape, dtype, after=None):
+            if isinstance(after, int):
+                return placed.tile(shape, dtype, name=name, offset=after, align_bytes=64)
             return sb.tile(shape, dtype, name=name, tag=after or name, align_bytes=64)
 
         def bank(name, index):
@@ -91,8 +94,8 @@ def tile_list_head_picks_prefix_memory_kernel(
         wo_rows = wo.rearrange("(b u t s) n -> b t u s n", b=PASSES, t=PACK, s=RUN)
         x_planes, wx_raw, wo_raw, tab = {}, {}, {}, {}
 
-        def load_x(a, i):
-            x_planes[a, i] = tile("x_%d_%d" % (a, i), [P, TX], F32)
+        def load_x(a, i, place=None):
+            x_planes[a, i] = tile("x_%d_%d" % (a, i), [P, TX], F32, place)
             nc.sync.dma_start(out=x_planes[a, i][:], in_=x_rows[a, i])
 
         def load_table(a):
@@ -168,11 +171,11 @@ def tile_list_head_picks_prefix_memory_kernel(
         load_x(1, 1)
         load_x(1, 2)
         load_wx(0, 1)
-        load_x(1, 3)
+        load_x(1, 3, LAST_PLANE)
         nc.vector.transpose(weight_columns[:], weight_pieces[:])
-        nc.vector.tensor_copy(
-            out=weight_spread[:].rearrange("p (b h s) -> p b h s", h=2, s=GROUP),
-            in_=weight_columns[:].rearrange("p (h b) -> p b h", h=2).unsqueeze(3).to_broadcast([P, S // QUAD, 2, GROUP]),
+        repeated = weight_columns[:].rearrange("p (h b) -> p b h", h=2).unsqueeze(3).to_broadcast([P, GROUP, 2, GROUP])
+        nc.vector.tensor_tensor(
+            weight_spread[:].rearrange("p (b h s) -> p b h s", h=2, s=GROUP), repeated, repeated, ALU.max
         )
         nc.vector.transpose(weights[:], weight_spread[:])
         for i in range(PACK):
@@ -364,8 +367,8 @@ def tile_list_head_picks_prefix_memory_kernel(
         wm_order(0, tile("wm_codes_0", [P, PASSES * 2 * PASS], U8, "wx_0_1"))
         xg_bf16[1] = interleave(on_scalar, "xg_bf16_1", picked[1][:], S)
         wm_order(1, placed.tile([P, PASSES * 2 * PASS], U8, name="wm_codes_1", offset=4 * S, align_bytes=64))
-        xg[0] = quantize("xg_0", xg_bf16[0], S, "x_1_2")
-        wx_quantize(0, 0, 0, "x_1_3")
+        xg[0] = quantize("xg_0", xg_bf16[0], S, LAST_PLANE)
+        wx_quantize(0, 0, 0, LAST_PLANE + 4 * S)
         wx_passes(0, 0, 0)
         wx_quantize(0, 1, 0, "weights")
         gather_codes(0, tile("v_codes_0", [P, S], U32, "wx_bf16_0_0_0"))

from contextlib import ExitStack

import concourse.mybir as mybir
from concourse.masks import make_identity

K, M, H, N, T, TX, S = 1024, 1024, 1024, 512, 2048, 1024, 512
FLOPS = 2 * S * (K * H + M * H + H * N)

F32 = mybir.dt.float32
BF16 = mybir.dt.bfloat16
I32 = mybir.dt.int32
U32 = mybir.dt.uint32
U16 = mybir.dt.uint16
U8 = mybir.dt.uint8
FP8X4 = mybir.dt.float8_e4m3fn_x4
FP4X4 = mybir.dt.float4_e2m1fn_x4
ALU = mybir.AluOpType
ACT = mybir.ActivationFunctionType

P = 128
PACK = 4
PASS = P * PACK
PASSES = 2
HALF = S // 2
RUN = 4
QUAD = 32
GROUP = 16
BO_ROW = P - QUAD - 1
B_ROW = P - 2 * PASSES
G_ROW = P - PASSES
LAST = PACK - 1
LAST_PLANE = 2 * 4 * PACK * S


def tile_list_head_picks_prefix_memory_kernel(
    tc, xT, wgt, offs2, tab_words, tab_scales, offs, wx, wm_words, wm_scales, b, g, wo, bo, out
):
    nc = tc.nc
    with ExitStack() as ctx:
        sb = ctx.enter_context(tc.tile_pool(name="sb", bufs=1))
        placed = ctx.enter_context(tc.tile_pool(name="placed", bufs=1))
        psum = ctx.enter_context(tc.psum_pool(name="psum", bufs=1))

        def tile(name, shape, dtype, after=None):
            if isinstance(after, int):
                return placed.tile(shape, dtype, name=name, offset=after, align_bytes=64)
            return sb.tile(shape, dtype, name=name, tag=after or name, align_bytes=64)

        def bank(name, index):
            return psum.tile([P, S], F32, name=name, tag="bank%d" % index)

        def quantize(name, source, columns, after=None, scales=None):
            codes = tile(name + "_codes", [P, columns], U32, after)
            if scales is None:
                scales = tile(name + "_scales", [P, columns], U8)
            nc.vector.quantize_mx(out=codes[:].bitcast(FP8X4), scales=scales[:], in_=source[:])
            return codes, scales

        def woven_view(woven):
            return woven[:].rearrange("p (c j i) -> p c i j", j=RUN, i=PACK)

        def planes_view(planes):
            return planes.rearrange("p i (c j) -> p c i j", j=RUN)

        def interleave(copy, name, planes, columns, after=None):
            woven = tile(name, [P, PACK * columns], BF16, after)
            copy(out=woven_view(woven), in_=planes_view(planes))
            return woven

        on_vector, on_scalar = nc.vector.tensor_copy, nc.scalar.copy

        tab_plane = placed.tile([P, T], U8, name="tab_plane", offset=0, align_bytes=64)
        v_scales_1 = tile("v_scales_1", [P, S], U8)
        wm_plane_raw = tile("wm_plane_raw", [P, PASSES * H], U8)
        wm_plane = tile("wm_plane", [P, PASSES * H], U8)
        rows = tile("rows", [P, PASS], F32)
        rows_dealt = tile("rows_dealt", [P, PASS], F32)
        identity = tile("identity", [P, P], F32)
        nc.vector.memset(tab_plane[:].bitcast(I32), 0)
        nc.vector.memset(wm_plane[:].bitcast(I32), 0)
        nc.vector.memset(rows[P - QUAD : B_ROW, :], 0.0)
        nc.vector.memset(rows_dealt[0:BO_ROW, :], 0.0)
        nc.vector.memset(v_scales_1[:].bitcast(I32), 0)
        make_identity(nc, identity[:])

        head_lists = sb.tile([P, S // 16], U16, name="head_lists")
        table_list = sb.tile([P, S // 16], U16, name="table_list")
        weights = tile("weights", [P, S], F32)
        weight_pieces = tile("weight_pieces", [P, QUAD], F32)
        weight_columns = tile("weight_columns", [P, QUAD], F32)
        weight_spread = tile("weight_spread", [P, S], F32)
        x_rows = xT.rearrange("(a p i) t -> a i p t", a=PASSES, i=PACK)
        wx_rows = wx.rearrange("(a p i) r -> a p i r", a=PASSES, i=PACK)
        wo_rows = wo.rearrange("(b u t s) n -> b t u s n", b=PASSES, t=PACK, s=RUN)
        x_planes, wx_raw, wo_raw, tab = {}, {}, {}, {}

        def load_x(a, i, place=None):
            x_planes[a, i] = tile("x_%d_%d" % (a, i), [P, TX], F32, place)
            nc.sync.dma_start(out=x_planes[a, i][:], in_=x_rows[a, i])

        def load_table(a):
            tab[a] = tile("tab_%d" % a, [P, T], U32)
            nc.sync.dma_start(
                out=tab[a][:].bitcast(I32), in_=tab_words[a].rearrange("p t i -> p (t i)").bitcast(I32)
            )

        def load_wx(hb, a):
            wx_raw[hb, a] = tile("wx_%d_%d" % (hb, a), [P, PACK, PASS], F32)
            nc.sync.dma_start(out=wx_raw[hb, a][:], in_=wx_rows[a][:, :, hb * PASS : (hb + 1) * PASS])

        def load_wo(hb):
            wo_raw[hb] = tile("wo_%d" % hb, [P, PACK, N], F32)
            for t in range(PACK):
                nc.sync.dma_start(out=wo_raw[hb][:, t, :], in_=wo_rows[hb, t])

        def load_table_scales(queue):
            for q in range(4):
                queue.dma_start(
                    out=tab_plane[32 * q : 32 * q + 8, :].bitcast(I32),
                    in_=tab_scales[:, 4 * q : 4 * q + 4, :].bitcast(I32),
                )

        def load_wm_scales(queue):
            for q in range(4):
                queue.dma_start(
                    out=wm_plane_raw[32 * q : 32 * q + 4, :].bitcast(I32).rearrange("r (a c) -> r a c", a=PASSES),
                    in_=wm_scales[:, 4 * q : 4 * q + 4, :].bitcast(I32).rearrange("a r c -> r a c"),
                )

        def load_rows(queue):
            queue.dma_start(out=rows[B_ROW:G_ROW, :], in_=b.rearrange("(h c) -> h c", h=PASSES))
            queue.dma_start(out=rows[G_ROW:P, :], in_=g.rearrange("(h c) -> h c", h=PASSES))
            queue.dma_start(out=rows_dealt[BO_ROW : BO_ROW + 1, :], in_=bo.rearrange("(h c) -> h c", h=1))

        wm_raw, wm_codes = {}, {}

        def load_wm():
            wm_raw[0] = tile("wm_raw", [P, PASSES, H // 2], I32)
            nc.sync.dma_start(out=wm_raw[0][:], in_=wm_words.bitcast(I32).rearrange("a p c -> p a c"))

        def wm_order(hb, codes):
            wm_codes[hb] = codes
            nc.scalar.copy(
                out=wm_codes[hb][:].bitcast(U32).rearrange("p (a t u w) -> p a u t w", t=PACK, u=32, w=2),
                in_=wm_raw[0][:]
                .bitcast(U32)[:, :, hb * PASS // 2 : (hb + 1) * PASS // 2]
                .rearrange("p a (u t w) -> p a u t w", t=PACK, w=2),
            )

        picked = {}

        def gather_x(a, i, after=None):
            if i == 0:
                picked[a] = placed.tile([P, PACK, S], F32, name="picked_%d" % a, offset=after, align_bytes=64)
            nc.vector.tensor_tensor(
                picked[a][:, i, :], x_planes[a, i][:].indirect(head_lists[:]), weights[:], ALU.mult
            )

        load_table_scales(nc.gpsimd)
        load_rows(nc.scalar)
        load_wm_scales(nc.scalar)
        nc.sync.dma_start(out=weight_pieces[:], in_=wgt.rearrange("(g s) (b r) -> g s b r", s=GROUP, r=QUAD)[:, 0])
        nc.sync.dma_start(head_lists[:], offs2)
        load_x(0, 0)
        load_x(0, 1)
        nc.sync.dma_start(table_list[:], offs)
        load_x(0, 2)
        load_x(0, 3)
        load_wx(0, 0)
        load_x(1, 0)
        load_x(1, 1)
        load_x(1, 2)
        load_wx(0, 1)
        load_x(1, 3, LAST_PLANE)
        nc.vector.transpose(weight_columns[:], weight_pieces[:])
        repeated = weight_columns[:].rearrange("p (h b) -> p b h", h=2).unsqueeze(3).to_broadcast([P, GROUP, 2, GROUP])
        nc.vector.tensor_tensor(
            weight_spread[:].rearrange("p (b h s) -> p b h s", h=2, s=GROUP), repeated, repeated, ALU.max
        )
        nc.vector.transpose(weights[:], weight_spread[:])
        for i in range(PACK):
            gather_x(0, i, 4 * PACK * S)
        v_scales_0 = tile("v_scales_0", [P, S], U8, "x_0_2")
        nc.vector.tensor_copy(v_scales_0[:], tab_plane[:].indirect(table_list[:]))
        nc.gpsimd.dma_start(out=v_scales_1[0:100, :].bitcast(I32), in_=v_scales_0[4:104, :].bitcast(I32))
        v_scales = [v_scales_0, v_scales_1]
        load_wm()
        load_table(0)
        load_table(1)
        load_wx(1, 0)
        load_wx(1, 1)
        load_wo(0)
        load_wo(1)

        nc.scalar.activation(
            rows_dealt[P - QUAD : P, :].rearrange("p (t u s) -> p u t s", t=PACK, s=RUN),
            rows[P - QUAD : P, :].rearrange("p (u t s) -> p u t s", t=PACK, s=RUN),
            ACT.Identity,
        )
        turned = bank("turned", 7)
        for t in range(PACK):
            nc.tensor.transpose(turned[:, t * P : (t + 1) * P], rows_dealt[:, t * P : (t + 1) * P], identity[:])
        consts = tile("consts", [P, 33, PACK], F32)
        nc.scalar.copy(out=consts[:], in_=turned[:].rearrange("p (t k) -> p k t", t=PACK)[:, BO_ROW:P, :])
        bias = {}
        for hb in range(PASSES):
            for half in range(2):
                bias[hb, half] = tile("bias_%d_%d" % (hb, half), [P, PACK], F32)
                nc.scalar.copy(out=bias[hb, half][:], in_=turned[:, B_ROW + hb : S : P])
        for q in range(4):
            live = slice(QUAD * q, QUAD * q + 4)
            nc.scalar.copy(
                out=wm_plane[live, :].bitcast(U32).rearrange("p (e t u) -> p e u t", t=PACK, u=QUAD),
                in_=wm_plane_raw[live, :].bitcast(U32).rearrange("p (e u t) -> p e u t", t=PACK, u=QUAD),
            )

        wx_bf16, wx_q, xg_bf16, xg, v_codes, z = {}, {}, {}, {}, {}, {}

        def wx_round(hb, a, first, count, copy, after=None):
            name = "wx_bf16_%d_%d_%d" % (hb, a, first)
            wx_bf16[hb, a, first] = tile(name, [P, count * PACK * P], BF16, after), count
            copy(
                out=wx_bf16[hb, a, first][0][:].rearrange("p (t u s i) -> p u t i s", t=count, s=RUN, i=PACK),
                in_=wx_raw[hb, a][:].rearrange("p i (u t s) -> p u t i s", t=PACK, s=RUN)[:, :, first : first + count],
            )

        def wx_quantize(hb, a, first, after=None):
            woven, count = wx_bf16[hb, a, first]
            wx_q[hb, a, first] = quantize("wx_%d_%d_%d" % (hb, a, first), woven, count * P, after), count

        def z_bank(hb, t):
            first = (hb, t) not in z
            if first:
                z[hb, t] = bank("z_%d_%d" % (hb, t), PACK * hb + t)
            return z[hb, t], first

        def wx_passes(hb, a, t0, stop=False):
            (codes, scales), count = wx_q[hb, a, t0]
            for c in range(count):
                acc, first = z_bank(hb, t0 + c)
                nc.tensor.matmul_mx(
                    out=acc[:],
                    lhsT=codes[:, c * P : (c + 1) * P].bitcast(FP8X4),
                    lhsT_scale=scales[:, c * P : (c + 1) * P],
                    rhs=xg[a][0][:].bitcast(FP8X4),
                    rhs_scale=xg[a][1][:],
                    start=first,
                    stop=stop,
                )

        def table_passes(hb, a, stop=False):
            for t in range(PACK):
                c0 = a * H + hb * PASS + t * P
                w0 = a * PASS + t * P
                acc, first = z_bank(hb, t)
                nc.tensor.matmul_mx(
                    out=acc[:],
                    lhsT=wm_codes[hb][:, 2 * w0 : 2 * (w0 + P)].bitcast(FP4X4),
                    lhsT_scale=wm_plane[:, c0 : c0 + P],
                    rhs=v_codes[a][:].bitcast(FP8X4),
                    rhs_scale=v_scales[a][:],
                    start=first,
                    stop=stop,
                )

        def gather_codes(a, codes):
            v_codes[a] = codes
            nc.vector.tensor_copy(v_codes[a][:], tab[a][:].indirect(table_list[:]))

        tanh, h_bf16, h = {}, {}, {}

        def activate(hb, half, tiles=range(PACK)):
            if (hb, half) not in tanh:
                tanh[hb, half] = tile("tanh_%d_%d" % (hb, half), [P, PACK, HALF], F32)
            for t in tiles:
                nc.scalar.activation(
                    tanh[hb, half][:, t, :],
                    z[hb, t][:, half * HALF : (half + 1) * HALF],
                    ACT.Tanh,
                    bias=bias[hb, half][:, t : t + 1],
                )

        def h_round(hb, half, after=None):
            h_bf16[hb, half] = tile("h_bf16_%d_%d" % (hb, half), [P, PACK * HALF], BF16, after)
            gain = consts[:, G_ROW - BO_ROW + hb, :].unsqueeze(1).unsqueeze(3).to_broadcast([P, HALF // RUN, PACK, RUN])
            nc.vector.tensor_tensor(woven_view(h_bf16[hb, half]), planes_view(tanh[hb, half][:]), gain, ALU.mult)

        def h_scale(hb, half, after):
            planes = tile("h_planes_%d_%d" % (hb, half), [P, PACK, HALF], BF16, after)
            for t in range(PACK):
                nc.scalar.activation(
                    planes[:, t, :],
                    tanh[hb, half][:, t, :],
                    ACT.Identity,
                    scale=consts[:, G_ROW - BO_ROW + hb, t : t + 1],
                )
            return planes

        def h_quantize(hb, half, after=None):
            h[hb, half] = quantize("h_%d_%d" % (hb, half), h_bf16[hb, half], HALF, after)

        wo_bf16, wo_q, y = {}, {}, {}

        def wo_round(hb, pair, copy, after=None):
            planes = wo_raw[hb][:, :, 2 * P * pair : 2 * P * (pair + 1)]
            wo_bf16[hb, pair] = interleave(copy, "wo_bf16_%d_%d" % (hb, pair), planes, 2 * P, after)

        def wo_tile_round(n, copy, after):
            planes = wo_raw[0][:, :, n * P : (n + 1) * P]
            wo_bf16[0, n] = interleave(copy, "wo_bf16_tile_%d" % n, planes, P, after)

        def wo_tile_quantize(n, after=None):
            codes, scales = quantize("wo_0_tile_%d" % n, wo_bf16[0, n], P, after)
            for half in range(2):
                if n != LAST:
                    y[n, half] = bank("y_%d_%d" % (n, half), PACK + 2 * half + n % 2)
                nc.tensor.matmul_mx(
                    out=y[n, half][:, 0:HALF],
                    lhsT=codes[:].bitcast(FP8X4),
                    lhsT_scale=scales[:],
                    rhs=h[0, half][0][:].bitcast(FP8X4),
                    rhs_scale=h[0, half][1][:],
                    start=(n != LAST),
                    stop=(n == LAST),
                )

        def wo_quantize(hb, pair, after=None):
            wo_q[hb, pair] = quantize("wo_%d_%d" % (hb, pair), wo_bf16[hb, pair], 2 * P, after)

        def wo_passes(hb, half, pair, tiles=range(2)):
            codes, scales = wo_q[hb, pair]
            for c in tiles:
                n = 2 * pair + c
                if (n, half) not in y:
                    y[n, half] = bank("y_%d_%d" % (n, half), PACK * pair + 2 * half + c)
                nc.tensor.matmul_mx(
                    out=y[n, half][:, 0:HALF],
                    lhsT=codes[:, c * P : (c + 1) * P].bitcast(FP8X4),
                    lhsT_scale=scales[:, c * P : (c + 1) * P],
                    rhs=h[hb, half][0][:].bitcast(FP8X4),
                    rhs_scale=h[hb, half][1][:],
                    start=(hb == 0 or n == LAST),
                    stop=(hb == 1 and n != LAST),
                )

        result = {}

        def add_bias(n, half, vector):
            if n not in result:
                result[n] = tile("result_%d" % n, [P, S], F32)
            target = result[n][:, half * HALF : (half + 1) * HALF]
            column = consts[:, 0, n : n + 1]
            if vector:
                nc.vector.tensor_scalar(target, y[n, half][:, 0:HALF], column, None, ALU.add)
            else:
                nc.scalar.activation(target, y[n, half][:, 0:HALF], ACT.Identity, bias=column)

        def store(n):
            nc.sync.dma_start(out=out[n * P : (n + 1) * P, :], in_=result[n][:])

        xg_bf16[0] = interleave(on_scalar, "xg_bf16_0", picked[0][:], S)
        wx_round(0, 0, 0, 4, on_scalar)
        gather_x(1, 0, 0)
        for i in range(1, PACK):
            gather_x(1, i)
        wx_round(0, 1, 0, 4, on_scalar, "wx_0_0")
        wm_order(0, tile("wm_codes_0", [P, PASSES * 2 * PASS], U8, "wx_0_1"))
        xg_bf16[1] = interleave(on_scalar, "xg_bf16_1", picked[1][:], S)
        wm_order(1, placed.tile([P, PASSES * 2 * PASS], U8, name="wm_codes_1", offset=4 * S, align_bytes=64))
        xg[0] = quantize("xg_0", xg_bf16[0], S, LAST_PLANE)
        wx_quantize(0, 0, 0, LAST_PLANE + 4 * S)
        wx_passes(0, 0, 0)
        wx_quantize(0, 1, 0, "weights")
        gather_codes(0, tile("v_codes_0", [P, S], U32, "wx_bf16_0_0_0"))
        table_passes(0, 0)
        xg[1] = quantize("xg_1", xg_bf16[1], S, "tab_0")
        wx_passes(0, 1, 0)
        gather_codes(1, placed.tile([P, S], U32, name="v_codes_1", offset=0, align_bytes=64))
        table_passes(0, 1, stop=True)
        table_passes(1, 1)
        table_passes(1, 0)
        activate(0, 0)
        activate(0, 1)

        wx_round(1, 0, 0, 2, on_vector, "xg_bf16_1")
        wx_round(1, 0, 2, 2, on_vector, "tab_1")
        wx_quantize(1, 0, 0)
        wx_passes(1, 0, 0)
        wx_quantize(1, 0, 2)
        wx_passes(1, 0, 2)
        h_round(0, 0, "xg_bf16_1")
        wx_round(1, 1, 0, 2, on_vector, "bias_0_0")
        wx_round(1, 1, 2, 2, on_scalar, "bias_0_1")
        scaled = h_scale(0, 1, "wx_1_1")
        h_quantize(0, 0)
        wx_quantize(1, 1, 0)
        wx_passes(1, 1, 0, stop=True)
        wx_quantize(1, 1, 2)
        wx_passes(1, 1, 2, stop=True)
        activate(1, 0)
        activate(1, 1)
        h_bf16[0, 1] = interleave(on_vector, "h_bf16_0_1", scaled[:], HALF, "bias_0_1")
        wo_round(0, 0, on_vector, "bias_0_0")
        h_quantize(0, 1)
        wo_tile_round(2, on_vector, "tanh_0_1")
        for t in range(2):
            codes, scales = wx_q[1, 1, 2][0]
            nc.tensor.matmul_mx(
                out=bank("warm_%d" % t, PACK + t)[:],
                lhsT=codes[:, t * P : (t + 1) * P].bitcast(FP8X4),
                lhsT_scale=scales[:, t * P : (t + 1) * P],
                rhs=xg[1][0][:].bitcast(FP8X4),
                rhs_scale=xg[1][1][:],
                start=True,
                stop=True,
            )
        h_round(1, 0)
        wo_quantize(0, 0, "bias_1_0")
        wo_passes(0, 0, 0)
        wo_passes(0, 1, 0)
        wo_round(1, 0, on_scalar, "bias_1_1")
        wo_round(1, 1, on_scalar, "tanh_1_0")
        h_quantize(1, 0)
        h_round(1, 1)
        wo_quantize(1, 0)
        wo_passes(1, 0, 0)
        h_quantize(1, 1)
        wo_passes(1, 1, 0)
        wo_tile_quantize(2, "tanh_1_1")
        wo_quantize(1, 1)
        for c in range(2):
            for half in range(2):
                wo_passes(1, half, 1, [c])
        add_bias(0, 0, False)
        add_bias(0, 1, False)
        store(0)
        wo_tile_round(3, on_scalar, "h_bf16_1_1")
        add_bias(1, 0, True)
        add_bias(1, 1, True)
        store(1)
        add_bias(2, 0, True)
        add_bias(2, 1, False)
        store(2)
        wo_tile_quantize(3)
        add_bias(3, 0, False)
        add_bias(3, 1, True)
        store(3)
